import numpy as np
import ml_dtypes


def mxq(x, axis, fmt="e4m3"):
    dtype, down = {"e4m3": (ml_dtypes.float8_e4m3fn, 7), "e5m2": (ml_dtypes.float8_e5m2, 14)}[fmt]
    v = np.moveaxis(np.asarray(x, np.float32).astype(ml_dtypes.bfloat16).astype(np.float64), axis, -1)
    blocks = v.reshape(v.shape[:-1] + (-1, 32))
    amax = np.abs(blocks).max(-1, keepdims=True)
    byte = np.maximum(np.where(amax > 0, np.frexp(amax)[1] - 1 + 127, 0) - down, 1)
    scale = np.exp2(byte - 127.0)
    codes = (blocks / scale).astype(np.float32).astype(dtype).astype(np.float64)
    return np.moveaxis((codes * scale).reshape(v.shape), -1, axis)


WIDE = False


def mx_kscale(k):
    if not WIDE:
        return np.ones(k)
    levels = np.array([10, -10, 5, -5, 0])
    if k % 512:
        return np.exp2(np.random.permutation(np.resize(levels, k // 32))).repeat(32)
    a = np.empty((k // 512, 16))
    for p in range(k // 512):
        a[p, :8] = np.random.permutation(np.resize(levels, 8))
        for g in range(8):
            far = levels[np.abs(levels - a[p, g]) >= 10]
            a[p, g + 8] = far[np.random.randint(len(far))]
    return np.exp2(a.ravel()).repeat(32)


BF16 = ml_dtypes.bfloat16


def bf(x):
    return np.asarray(x, np.float32).astype(BF16)


def f64(x):
    return np.asarray(x).astype(np.float64)

def planes(Y):
    n, m = Y.shape
    b = f64(bf(Y)).reshape(n // 32, 32, m)
    amax = np.abs(b).max(1)
    byte = np.clip(np.where(amax > 0, np.frexp(amax)[1] - 1 + 127 - 7, 1), 1, 254)
    codes = (b * np.exp2(127.0 - byte)[:, None, :]).reshape(n, m).astype(np.float32).astype(ml_dtypes.float8_e4m3fn).view(np.uint8)
    words = codes.reshape(n // 512, 128, 4, m).transpose(0, 1, 3, 2)
    return np.ascontiguousarray(words), np.ascontiguousarray(byte.astype(np.uint8).reshape(n // 512, 16, m))


M, K, N, E, R, Q = 1024, 1536, 2048, 16, 32, 32

LEVELS = np.array([-6.0, -4.0, -3.0, -2.0, -1.5, -1.0, -0.5, 0.0, 0.5, 1.0, 1.5, 2.0, 3.0, 4.0, 6.0])

def setup_inputs():
    rn = np.random.randn
    s = mx_kscale(K)
    t = mx_kscale(E * R)
    step = np.repeat(np.exp(0.3 * rn(K // Q, N)), Q, axis=0) / (3.0 * np.sqrt(K))
    return {
        "x": bf(rn(M, K) * s),
        "w": bf(np.random.choice(LEVELS, size=(K, N)) * step / s[:, None]),
        "u": bf(rn(M, E * R) * t),
        "mix": bf(np.random.uniform(0.2, 1.8, size=(M, E))),
        "b": bf(0.7 * rn(E * R, N) / np.sqrt(E * R) / t[:, None]),
        "mag": bf(np.exp(0.8 * rn(N))),
        "act": bf(rn(M, N)),
    }

def reference(x, w, u, mix, b, mag, act):
    x, w, u, mix = f64(x), f64(w), f64(u), f64(mix)
    b, mag, act = f64(b), f64(mag), f64(act)
    h = (u.reshape(M, E, R) * mix[:, :, None]).reshape(M, E * R)
    base = mxq(x, 1, "e4m3") @ mxq(w, 0, "e4m3")
    corr = mxq(h, 1, "e4m3") @ mxq(b, 0, "e4m3")
    y = act * (mag * (base + corr))
    Y = y.reshape(M, N).T
    words, scales = planes(Y)
    return y, words, scales

@@ -1,0 +1,344 @@
+from contextlib import ExitStack
+
+import concourse.mybir as mybir
+from concourse.masks import make_identity
+
+M, K, N, E, R = 1024, 1536, 2048, 16, 32
+FLOPS = 2 * M * (K + E * R) * N
+
+F32 = mybir.dt.float32
+BF16 = mybir.dt.bfloat16
+U32 = mybir.dt.uint32
+I32 = mybir.dt.int32
+U8 = mybir.dt.uint8
+FP8X4 = mybir.dt.float8_e4m3fn_x4
+MULT = mybir.AluOpType.mult
+
+P = 128
+G = 512
+PASSES = 4
+CHUNKS = N // G
+PAIRS = M // (2 * P)
+STEPS = CHUNKS * PAIRS
+V_HEAD = 320
+V_FIRST = 0
+V_MID = 128
+Y_BUFS = 11
+PLANES = (0, 0, 0, 0, 0, 1, 1, 1, 1, 1, 1, 1, 2, 2, 2, 1, 1, 1)
+V_CAST = (15,)
+STORE_LAG = 4
+
+
+def tile_frozen_fp4_adapter_mix_g1_kernel(tc, x, w, u, mix, b, mag, act, out_0, out_1, out_2):
+    nc = tc.nc
+    with ExitStack() as ctx:
+        sb = ctx.enter_context(tc.tile_pool(name="sb", bufs=1))
+        ps = ctx.enter_context(tc.psum_pool(name="ps", bufs=4))
+        ctx.enter_context(tc.manual_schedule())
+
+        ident = sb.tile([P, P], F32, name="ident")
+        mag_rows = sb.tile([P, 16], BF16, name="mag_rows")
+        mag_all = sb.tile([P, N], BF16, name="mag_all")
+        mix_rows = sb.tile([P, 2 * PAIRS, E], BF16, name="mix_rows")
+        mix_twice = sb.tile([P, 2 * PAIRS * E, 2], BF16, name="mix_twice")
+        y_scales = sb.tile([P, M], U8, name="y_scales", align_bytes=64)
+        words_out = out_1.rearrange("g p m t -> g p (m t)").bitcast(I32)
+        scales_out = out_2.bitcast(I32)
+
+        x_raw, u_raw, h, act_sb, w_raw, w_side, w_mx, x_side, x_mx = {}, {}, {}, {}, {}, {}, {}, {}, {}
+        gate, acc, y, y_bf, y_bank, y_side, y_codes, x_bank = {}, {}, {}, {}, {}, {}, {}, {}
+
+        def load_w(unit):
+            g, c = divmod(unit, PASSES)
+            rows = w[c * G : (c + 1) * G, :] if c < PASSES - 1 else b
+            t = sb.tile([P, 4, G], BF16, name="w_raw", bufs=8)
+            nc.sync.dma_start(out=t[:], in_=rows[:, g * G : (g + 1) * G].rearrange("(p j) n -> p j n", j=4))
+            w_raw[unit] = t
+
+        def load_x(a):
+            t = sb.tile([P, K], BF16, name="x_raw", bufs=6)
+            nc.sync.dma_start(out=t[:], in_=x[a * P : (a + 1) * P, :])
+            x_raw[a] = t
+
+        def load_u(pair):
+            t = sb.tile([P, 2, G], BF16, name="u_raw", bufs=4)
+            nc.sync.dma_start(out=t[:], in_=u[pair * 2 * P : (pair + 1) * 2 * P, :].rearrange("(a p) r -> p a r", p=P))
+            u_raw[pair] = t
+
+        def load_act(j):
+            g, pair = divmod(j, PAIRS)
+            t = sb.tile([P, 2, G], BF16, name="act_first", bufs=4)
+            rows = act[pair * 2 * P : (pair + 1) * 2 * P, g * G : (g + 1) * G]
+            nc.sync.dma_start(out=t[:], in_=rows.rearrange("(a p) n -> p a n", p=P))
+            act_sb[j] = t[:]
+
+        def load_act_chunk(g):
+            t = sb.tile([P, 2 * PAIRS, G], BF16, name="act_chunk", bufs=2)
+            nc.sync.dma_start(out=t[:], in_=act[:, g * G : (g + 1) * G].rearrange("(a p) n -> p a n", p=P))
+            for pair in range(PAIRS):
+                act_sb[g * PAIRS + pair] = t[:, 2 * pair : 2 * pair + 2, :]
+
+        def spread_mag():
+            pairs = mag_rows[:].bitcast(F32)
+            dst = mag_all[:].bitcast(F32).rearrange("q (p k i) -> q k p i", k=2, i=4)
+            for k in range(2):
+                bank = ps.tile([P, 4, P], F32, name="turn")
+                for i in range(4):
+                    col = 4 * k + i
+                    nc.tensor.transpose(bank[:, i, :], pairs[:, col : col + 1].to_broadcast([P, P]), ident[:])
+                nc.scalar.copy(out=dst[:, k], in_=bank[:].rearrange("q i p -> q p i"))
+
+        def weigh(pair):
+            t = sb.tile([P, 2 * G], BF16, name="h", bufs=2)
+            rows = slice(pair * 2 * E, (pair + 1) * 2 * E)
+            nc.vector.tensor_tensor(
+                out=t[:].rearrange("p (e r i) -> p e r i", r=R // 2, i=2),
+                in0=u_raw[pair][:].rearrange("p a (e r i) -> p (a e) r i", r=R // 2, i=2),
+                in1=mix_twice[:, rows, :].unsqueeze(2).to_broadcast([P, 2 * E, R // 2, 2]),
+                op=MULT,
+            )
+            h[pair] = t
+
+        def interleave_w(unit, eng, lo, hi):
+            if unit not in w_side:
+                w_side[unit] = sb.tile([P, G, 4], BF16, name="w_side", bufs=3, align_bytes=64)
+            if hi > lo:
+                dst = w_side[unit][:, lo:hi, :].rearrange("p (c i) t -> p c t i", i=4)
+                src = w_raw[unit][:, :, lo:hi].rearrange("p t (c i) -> p c t i", i=4)
+                if eng == "vector":
+                    nc.vector.tensor_copy(out=dst, in_=src)
+                else:
+                    nc.scalar.copy(out=dst, in_=src)
+
+        def quantize(src, name, bufs):
+            codes = sb.tile([P, G], U32, name=name + "_codes", bufs=bufs, align_bytes=64)
+            scales = sb.tile([P, G], U8, name=name + "_scales", bufs=bufs, align_bytes=64)
+            nc.vector.quantize_mx(out=codes[:].bitcast(FP8X4), scales=scales[:], in_=src)
+            return codes, scales
+
+        def quantize_w(unit):
+            w_mx[unit] = quantize(w_side[unit][:].rearrange("p n t -> p (n t)"), "w", 8)
+
+        def turn_x(a, half):
+            bank = ps.tile([P, 2, 2, P], F32, name="turn")
+            for i in range(2):
+                c = 2 * half + i
+                if c < PASSES - 1:
+                    pairs = x_raw[a][:].bitcast(F32)[:, c * 256 : (c + 1) * 256]
+                else:
+                    pairs = h[a // 2][:].bitcast(F32)[:, (a % 2) * 256 : (a % 2 + 1) * 256]
+                for e in range(2):
+                    nc.tensor.transpose(bank[:, i, e, :], pairs[:, e::2], ident[:])
+            x_bank[a, half] = bank
+
+        def empty_x(a, half):
+            if half == 0:
+                x_side[a] = sb.tile([P, PASSES * P * 4], BF16, name="x_side", bufs=2, align_bytes=64)
+            dst = x_side[a][:].bitcast(F32).rearrange("p (c r e) -> p c r e", c=PASSES, e=2)
+            nc.scalar.copy(out=dst[:, 2 * half : 2 * half + 2], in_=x_bank[a, half][:].rearrange("p c e r -> p c r e"))
+
+        def quantize_x(a):
+            x_mx[a] = quantize(x_side[a][:], "x", 2 * PAIRS)
+
+        def make_gate(j):
+            g = j // PAIRS
+            t = sb.tile([P, 2, G], F32, name="gate", bufs=2)
+            nc.vector.tensor_tensor(
+                out=t[:],
+                in0=act_sb[j],
+                in1=mag_all[:, g * G : (g + 1) * G].unsqueeze(1).to_broadcast([P, 2, G]),
+                op=MULT,
+            )
+            gate[j] = t
+
+        def multiply(j, tiles):
+            g, pair = divmod(j, PAIRS)
+            for i in tiles:
+                acc[j, i] = ps.tile([P, G], F32, name="acc")
+            for c in range(PASSES):
+                w_codes, w_scales = w_mx[g * PASSES + c]
+                for i in tiles:
+                    x_codes, x_scales = x_mx[2 * pair + i]
+                    cols = slice(c * P, (c + 1) * P)
+                    nc.tensor.matmul_mx(
+                        out=acc[j, i][:],
+                        lhsT=x_codes[:, cols].bitcast(FP8X4),
+                        lhsT_scale=x_scales[:, cols],
+                        rhs=w_codes[:].bitcast(FP8X4),
+                        rhs_scale=w_scales[:],
+                        start=(c == 0),
+                        stop=(c == PASSES - 1),
+                    )
+
+        def finish(j, i):
+            if i == 0:
+                y[j] = sb.tile([P, 2, G], F32, name="y", bufs=Y_BUFS)
+            nc.vector.tensor_tensor(out=y[j][:, i, :], in0=acc[j, i][:], in1=gate[j][:, i, :], op=MULT)
+
+        def store_y(j):
+            g, pair = divmod(j, PAIRS)
+            rows = out_0[pair * 2 * P : (pair + 1) * 2 * P, g * G : (g + 1) * G]
+            nc.sync.dma_start(out=rows.rearrange("(a p) n -> p a n", p=P), in_=y[j][:])
+
+        def round_y(j):
+            t = sb.tile([P, 2, 2, P, 2], BF16, name="y_bf", bufs=3)
+            src = y[j][:].rearrange("q a (p e i) -> q a e p i", e=2, i=2)
+            if j in V_CAST:
+                nc.vector.tensor_copy(out=t[:], in_=src)
+            else:
+                nc.scalar.copy(out=t[:], in_=src)
+            y_bf[j] = t
+
+        def turn_y(j):
+            bank = ps.tile([P, 2, 2, P], F32, name="turn")
+            pairs = y_bf[j][:].rearrange("q a e p i -> q (a e p i)").bitcast(F32)
+            for a in range(2):
+                for e in range(2):
+                    s = (2 * a + e) * P
+                    nc.tensor.transpose(bank[:, a, e, :], pairs[:, s : s + P], ident[:])
+            y_bank[j] = bank
+
+        def empty_y(j):
+            t = sb.tile([P, 2 * P * 4], BF16, name="y_side", bufs=3, align_bytes=64)
+            dst = t[:].bitcast(F32).rearrange("p (a r e) -> p a r e", a=2, e=2)
+            nc.scalar.copy(out=dst, in_=y_bank[j][:].rearrange("p a e r -> p a r e"))
+            y_side[j] = t
+
+        def quantize_y(j):
+            g, pair = divmod(j, PAIRS)
+            if pair == 0:
+                y_codes[g] = sb.tile([P, M], U32, name="y_codes", bufs=3, align_bytes=64)
+            cols = slice(pair * 2 * P, (pair + 1) * 2 * P)
+            nc.vector.quantize_mx(out=y_codes[g][:, cols].bitcast(FP8X4), scales=y_scales[4 * g :, cols], in_=y_side[j][:])
+
+        def store_words(g, lo, hi):
+            nc.sync.dma_start(out=words_out[g, :, lo:hi], in_=y_codes[g][:, lo:hi].bitcast(I32))
+
+        def store_scales():
+            for q in range(4):
+                nc.sync.dma_start(out=scales_out[:, 4 * q : 4 * q + 4, :], in_=y_scales[32 * q : 32 * q + 16, :].bitcast(I32))
+
+        make_identity(nc, ident[:])
+        load_w(0)
+        nc.sync.dma_start(out=mix_rows[:], in_=mix.rearrange("(a p) e -> p a e", p=P))
+        nc.sync.dma_start(out=mag_rows[:], in_=mag.rearrange("(p c) -> p c", p=P))
+        load_x(0)
+        load_u(0)
+        load_w(1)
+        load_w(2)
+        load_w(3)
+        load_x(1)
+        load_act(0)
+        for pair in range(1, PAIRS):
+            load_u(pair)
+            load_x(2 * pair)
+            load_w(PASSES + pair - 1)
+            load_x(2 * pair + 1)
+            load_act(pair)
+        load_w(2 * PASSES - 1)
+        load_w(2 * PASSES)
+        load_act_chunk(1)
+
+        def share_w(unit, cols):
+            interleave_w(unit, "scalar", cols, G)
+            interleave_w(unit, "vector", 0, cols)
+
+        def prepare_x(a):
+            for half in range(2):
+                turn_x(a, half)
+                empty_x(a, half)
+
+        share_w(0, V_HEAD)
+        nc.vector.tensor_copy(
+            out=mix_twice[:],
+            in_=mix_rows[:].rearrange("p a e -> p (a e)").unsqueeze(2).to_broadcast([P, 2 * PAIRS * E, 2]),
+        )
+        quantize_w(0)
+        weigh(0)
+        prepare_x(0)
+        share_w(1, V_HEAD)
+        quantize_x(0)
+        quantize_w(1)
+        spread_mag()
+        share_w(2, V_HEAD)
+        quantize_w(2)
+        share_w(3, V_HEAD)
+        quantize_w(3)
+
+        for a in range(2 * PAIRS):
+            j, i = divmod(a, 2)
+            unit = PASSES + j
+            if i == 1 and j > 0:
+                load_w(unit + PASSES)
+            if a + 1 < 2 * PAIRS:
+                prepare_x(a + 1)
+            multiply(j, (i,))
+            if a == 0:
+                make_gate(0)
+            else:
+                finish(*divmod(a - 1, 2))
+            lo, hi = (V_FIRST, (V_FIRST + G) // 2) if i == 0 else ((V_FIRST + G) // 2, G)
+            interleave_w(unit, "scalar", lo, hi)
+            if i == 0:
+                if j + 1 < PAIRS:
+                    weigh(j + 1)
+                if j > 0:
+                    quantize_w(unit - 1)
+            else:
+                interleave_w(unit, "vector", 0, V_FIRST)
+                make_gate(j + 1)
+            if a + 1 < 2 * PAIRS:
+                quantize_x(a + 1)
+        load_act_chunk(2)
+
+        plan = {}
+        p = 0
+        for j in range(len(PLANES) + 1):
+            n = PLANES[j] if j < len(PLANES) else 0
+            plan[j] = list(range(p, p + n))
+            p = p + n
+        assert p == STEPS
+        stored = 0
+        for j in range(PAIRS, len(PLANES) + 1):
+            unit = j + PASSES
+            has_w = unit < CHUNKS * PASSES
+            if unit + PASSES < CHUNKS * PASSES:
+                load_w(unit + PASSES)
+            if j == 2 * PAIRS:
+                load_act_chunk(3)
+            if unit - 1 < CHUNKS * PASSES:
+                quantize_w(unit - 1)
+            if j < STEPS:
+                multiply(j, (0, 1))
+            if j <= STEPS:
+                if j > PAIRS:
+                    finish(j - 1, 0)
+                finish(j - 1, 1)
+            todo = list(plan[j - 1])
+            for q in plan[j]:
+                round_y(q)
+                if todo:
+                    empty_y(todo.pop(0))
+            for q in todo:
+                empty_y(q)
+            for q in plan[j]:
+                turn_y(q)
+            if has_w:
+                share_w(unit, V_MID)
+            if j + 1 < STEPS:
+                make_gate(j + 1)
+            for q in plan[j - 1]:
+                quantize_y(q)
+            upto = min(STEPS, j, j - STORE_LAG + 1 + max(0, j - 2 * PAIRS))
+            while stored < upto:
+                store_y(stored)
+                stored = stored + 1
+            for q in plan[j - 1]:
+                g, pair = divmod(q, PAIRS)
+                if g < CHUNKS - 1 and pair == PAIRS - 1:
+                    store_words(g, 0, M)
+                if g == CHUNKS - 1 and pair == PAIRS - 2:
+                    store_words(g, 0, M - 2 * P)
+                if g == CHUNKS - 1 and pair == PAIRS - 1:
+                    store_words(g, M - 2 * P, M)
+                    store_scales()

@@ -13,6 +13,7 @@ I32 = mybir.dt.int32
 U8 = mybir.dt.uint8
 FP8X4 = mybir.dt.float8_e4m3fn_x4
 MULT = mybir.AluOpType.mult
+ADD = mybir.AluOpType.add
 
 P = 128
 G = 512
@@ -22,10 +23,18 @@ PAIRS = M // (2 * P)
 STEPS = CHUNKS * PAIRS
 V_HEAD = 320
 V_FIRST = 0
-V_MID = 128
-Y_BUFS = 11
-PLANES = (0, 0, 0, 0, 0, 1, 1, 1, 1, 1, 1, 1, 2, 2, 2, 1, 1, 1)
-V_CAST = (15,)
+V_MID = 320
+WIDE_FROM = 8
+SPLIT0 = 0
+G_COLS = 0
+V_EVEN = 0
+G_GATE = 1
+G_CAST = ()
+V_8 = 0
+Y_BUFS = 8
+PLANE_START = 6
+DOUBLE_FROM = 12
+V_CAST = (11, 13)
 STORE_LAG = 4
 
 
@@ -47,21 +56,27 @@ def tile_frozen_fp4_adapter_mix_g1_kernel(tc, x, w, u, mix, b, mag, act, out_0, 
 
         x_raw, u_raw, h, act_sb, w_raw, w_side, w_mx, x_side, x_mx = {}, {}, {}, {}, {}, {}, {}, {}, {}
         gate, acc, y, y_bf, y_bank, y_side, y_codes, x_bank = {}, {}, {}, {}, {}, {}, {}, {}
+        w_whole, act_two, y_whole = {}, {}, {}
 
         def load_w(unit):
             g, c = divmod(unit, PASSES)
             rows = w[c * G : (c + 1) * G, :] if c < PASSES - 1 else b
-            t = sb.tile([P, 4, G], BF16, name="w_raw", bufs=8)
-            nc.sync.dma_start(out=t[:], in_=rows[:, g * G : (g + 1) * G].rearrange("(p j) n -> p j n", j=4))
+            t = sb.tile([P, 4, G], BF16, name="w_raw", bufs=6)
+            src = rows[:, g * G : (g + 1) * G].rearrange("(p j) n -> p j n", j=4)
+            if unit == 0 and SPLIT0:
+                nc.sync.dma_start(out=t[:, :, :SPLIT0], in_=src[:, :, :SPLIT0])
+                nc.sync.dma_start(out=t[:, :, SPLIT0:], in_=src[:, :, SPLIT0:])
+            else:
+                nc.sync.dma_start(out=t[:], in_=src)
             w_raw[unit] = t
 
         def load_x(a):
-            t = sb.tile([P, K], BF16, name="x_raw", bufs=6)
+            t = sb.tile([P, K], BF16, name="x_raw", bufs=5)
             nc.sync.dma_start(out=t[:], in_=x[a * P : (a + 1) * P, :])
             x_raw[a] = t
 
         def load_u(pair):
-            t = sb.tile([P, 2, G], BF16, name="u_raw", bufs=4)
+            t = sb.tile([P, 2, G], BF16, name="u_raw", bufs=3)
             nc.sync.dma_start(out=t[:], in_=u[pair * 2 * P : (pair + 1) * 2 * P, :].rearrange("(a p) r -> p a r", p=P))
             u_raw[pair] = t
 
@@ -77,6 +92,7 @@ def tile_frozen_fp4_adapter_mix_g1_kernel(tc, x, w, u, mix, b, mag, act, out_0, 
             nc.sync.dma_start(out=t[:], in_=act[:, g * G : (g + 1) * G].rearrange("(a p) n -> p a n", p=P))
             for pair in range(PAIRS):
                 act_sb[g * PAIRS + pair] = t[:, 2 * pair : 2 * pair + 2, :]
+                act_two[g * PAIRS + pair] = t[:, 2 * pair : min(2 * pair + 4, 2 * PAIRS), :]
 
         def spread_mag():
             pairs = mag_rows[:].bitcast(F32)
@@ -101,23 +117,38 @@ def tile_frozen_fp4_adapter_mix_g1_kernel(tc, x, w, u, mix, b, mag, act, out_0, 
 
         def interleave_w(unit, eng, lo, hi):
             if unit not in w_side:
-                w_side[unit] = sb.tile([P, G, 4], BF16, name="w_side", bufs=3, align_bytes=64)
+                if unit < WIDE_FROM:
+                    t = sb.tile([P, G, 4], BF16, name="w_side", tag="side%d" % (unit % 3), align_bytes=64)
+                    w_side[unit] = t[:]
+                else:
+                    t = sb.tile([P, 2, G, 4], BF16, name="w_side", tag="side%d" % ((unit // 2 + 1) % 3), align_bytes=64)
+                    w_side[unit], w_side[unit + 1] = t[:, 0], t[:, 1]
+                w_whole[unit] = t
             if hi > lo:
                 dst = w_side[unit][:, lo:hi, :].rearrange("p (c i) t -> p c t i", i=4)
                 src = w_raw[unit][:, :, lo:hi].rearrange("p t (c i) -> p c t i", i=4)
                 if eng == "vector":
                     nc.vector.tensor_copy(out=dst, in_=src)
-                else:
+                elif eng == "scalar":
                     nc.scalar.copy(out=dst, in_=src)
+                else:
+                    src = w_raw[unit][:, :, lo:hi].rearrange("p t n -> p n t")
+                    nc.gpsimd.tensor_scalar(out=w_side[unit][:, lo:hi, :], in0=src, scalar1=1.0, scalar2=0.0, op0=MULT, op1=ADD)
 
-        def quantize(src, name, bufs):
-            codes = sb.tile([P, G], U32, name=name + "_codes", bufs=bufs, align_bytes=64)
-            scales = sb.tile([P, G], U8, name=name + "_scales", bufs=bufs, align_bytes=64)
+        def quantize(src, name, bufs, width):
+            codes = sb.tile([P, width], U32, name=name + "_codes", bufs=bufs, align_bytes=64)
+            scales = sb.tile([P, width], U8, name=name + "_scales", bufs=bufs, align_bytes=64)
             nc.vector.quantize_mx(out=codes[:].bitcast(FP8X4), scales=scales[:], in_=src)
             return codes, scales
 
         def quantize_w(unit):
-            w_mx[unit] = quantize(w_side[unit][:].rearrange("p n t -> p (n t)"), "w", 8)
+            if unit < WIDE_FROM:
+                codes, scales = quantize(w_whole[unit][:].rearrange("p n t -> p (n t)"), "w", 8, G)
+                w_mx[unit] = codes[:], scales[:]
+            else:
+                codes, scales = quantize(w_whole[unit][:].rearrange("p c n t -> p (c n t)"), "w2", 4, 2 * G)
+                w_mx[unit] = codes[:, :G], scales[:, :G]
+                w_mx[unit + 1] = codes[:, G:], scales[:, G:]
 
         def turn_x(a, half):
             bank = ps.tile([P, 2, 2, P], F32, name="turn")
@@ -138,18 +169,22 @@ def tile_frozen_fp4_adapter_mix_g1_kernel(tc, x, w, u, mix, b, mag, act, out_0, 
             nc.scalar.copy(out=dst[:, 2 * half : 2 * half + 2], in_=x_bank[a, half][:].rearrange("p c e r -> p c r e"))
 
         def quantize_x(a):
-            x_mx[a] = quantize(x_side[a][:], "x", 2 * PAIRS)
+            x_mx[a] = quantize(x_side[a][:], "x", 2 * PAIRS, G)
 
-        def make_gate(j):
+        def make_gate(j, n, eng=nc.vector):
             g = j // PAIRS
-            t = sb.tile([P, 2, G], F32, name="gate", bufs=2)
-            nc.vector.tensor_tensor(
+            if eng is nc.vector:
+                t = sb.tile([P, 2 * n, G], F32, name="gate", bufs=2)
+            else:
+                t = sb.tile([P, 2 * n, G], F32, name="gate_g", tag="side%d" % ((j + 3) // 2 % 3), align_bytes=64)
+            eng.tensor_tensor(
                 out=t[:],
-                in0=act_sb[j],
-                in1=mag_all[:, g * G : (g + 1) * G].unsqueeze(1).to_broadcast([P, 2, G]),
+                in0=act_sb[j] if n == 1 else act_two[j],
+                in1=mag_all[:, g * G : (g + 1) * G].unsqueeze(1).to_broadcast([P, 2 * n, G]),
                 op=MULT,
             )
-            gate[j] = t
+            for k in range(n):
+                gate[j + k] = t[:, 2 * k : 2 * k + 2, :]
 
         def multiply(j, tiles):
             g, pair = divmod(j, PAIRS)
@@ -164,8 +199,8 @@ def tile_frozen_fp4_adapter_mix_g1_kernel(tc, x, w, u, mix, b, mag, act, out_0, 
                         out=acc[j, i][:],
                         lhsT=x_codes[:, cols].bitcast(FP8X4),
                         lhsT_scale=x_scales[:, cols],
-                        rhs=w_codes[:].bitcast(FP8X4),
-                        rhs_scale=w_scales[:],
+                        rhs=w_codes.bitcast(FP8X4),
+                        rhs_scale=w_scales,
                         start=(c == 0),
                         stop=(c == PASSES - 1),
                     )
@@ -180,36 +215,69 @@ def tile_frozen_fp4_adapter_mix_g1_kernel(tc, x, w, u, mix, b, mag, act, out_0, 
             rows = out_0[pair * 2 * P : (pair + 1) * 2 * P, g * G : (g + 1) * G]
             nc.sync.dma_start(out=rows.rearrange("(a p) n -> p a n", p=P), in_=y[j][:])
 
-        def round_y(j):
-            t = sb.tile([P, 2, 2, P, 2], BF16, name="y_bf", bufs=3)
-            src = y[j][:].rearrange("q a (p e i) -> q a e p i", e=2, i=2)
-            if j in V_CAST:
-                nc.vector.tensor_copy(out=t[:], in_=src)
+        def store_tile(i):
+            a = 2 * PAIRS - 2 + i
+            nc.sync.dma_start(out=out_0[a * P : (a + 1) * P, N - G :], in_=y[STEPS - 1][:, i, :])
+
+        def round_y(j, eng):
+            if eng == "gpsimd":
+                t = sb.tile([P, 2, 2 * P, 2], BF16, name="y_bf_g", tag="side0", align_bytes=64)
             else:
+                t = sb.tile([P, 2, 2 * P, 2], BF16, name="y_bf", bufs=3)
+            src = y[j][:].rearrange("q a (p e i) -> q e (a p) i", e=2, i=2)
+            if eng == "vector":
+                nc.vector.tensor_copy(out=t[:], in_=src)
+            elif eng == "scalar":
                 nc.scalar.copy(out=t[:], in_=src)
+            else:
+                nc.gpsimd.tensor_scalar(out=t[:], in0=src, scalar1=1.0, scalar2=0.0, op0=MULT, op1=ADD)
             y_bf[j] = t
 
         def turn_y(j):
             bank = ps.tile([P, 2, 2, P], F32, name="turn")
-            pairs = y_bf[j][:].rearrange("q a e p i -> q (a e p i)").bitcast(F32)
+            pairs = y_bf[j][:].rearrange("q e r i -> q (e r i)").bitcast(F32)
             for a in range(2):
                 for e in range(2):
-                    s = (2 * a + e) * P
+                    s = (2 * e + a) * P
                     nc.tensor.transpose(bank[:, a, e, :], pairs[:, s : s + P], ident[:])
             y_bank[j] = bank
 
         def empty_y(j):
-            t = sb.tile([P, 2 * P * 4], BF16, name="y_side", bufs=3, align_bytes=64)
-            dst = t[:].bitcast(F32).rearrange("p (a r e) -> p a r e", a=2, e=2)
+            if j % 2 == 0:
+                y_whole[j] = sb.tile([P, 2, 2 * P * 4], BF16, name="y_side", bufs=3, align_bytes=64)
+            t = y_whole[j - j % 2][:, j % 2, :]
+            dst = t.bitcast(F32).rearrange("p (a r e) -> p a r e", a=2, e=2)
             nc.scalar.copy(out=dst, in_=y_bank[j][:].rearrange("p a e r -> p a r e"))
-            y_side[j] = t
 
-        def quantize_y(j):
+        def quantize_y(j, n):
             g, pair = divmod(j, PAIRS)
             if pair == 0:
-                y_codes[g] = sb.tile([P, M], U32, name="y_codes", bufs=3, align_bytes=64)
-            cols = slice(pair * 2 * P, (pair + 1) * 2 * P)
-            nc.vector.quantize_mx(out=y_codes[g][:, cols].bitcast(FP8X4), scales=y_scales[4 * g :, cols], in_=y_side[j][:])
+                y_codes[g] = sb.tile([P, M], U32, name="y_codes", bufs=2, align_bytes=64)
+            cols = slice(pair * 2 * P, (pair + n) * 2 * P)
+            src = y_whole[j - j % 2][:, j % 2 : j % 2 + n, :].rearrange("p k v -> p (k v)")
+            nc.vector.quantize_mx(out=y_codes[g][:, cols].bitcast(FP8X4), scales=y_scales[4 * g :, cols], in_=src)
+
+        def last_round(i):
+            j = STEPS - 1
+            t = sb.tile([P, 2, P, 2], BF16, name="y_last", tag="y_bf", bufs=3)
+            nc.vector.tensor_copy(out=t[:], in_=y[j][:, i, :].rearrange("q (p e i) -> q e p i", e=2, i=2))
+            bank = ps.tile([P, 2, P], F32, name="turn")
+            pairs = t[:].rearrange("q e r i -> q (e r i)").bitcast(F32)
+            for e in range(2):
+                nc.tensor.transpose(bank[:, e, :], pairs[:, e * P : (e + 1) * P], ident[:])
+            y_bank[j, i] = bank
+
+        def last_empty(i):
+            j = STEPS - 1
+            dst = y_whole[j - 1][:, 1, i * 4 * P : (i + 1) * 4 * P].bitcast(F32).rearrange("p (r e) -> p r e", e=2)
+            nc.scalar.copy(out=dst, in_=y_bank[j, i][:].rearrange("p e r -> p r e"))
+
+        def last_quantize(i):
+            j = STEPS - 1
+            cols = slice(M - (2 - i) * P, M - (1 - i) * P)
+            src = y_whole[j - 1][:, 1, i * 4 * P : (i + 1) * 4 * P]
+            g = CHUNKS - 1
+            nc.vector.quantize_mx(out=y_codes[g][:, cols].bitcast(FP8X4), scales=y_scales[4 * g :, cols], in_=src)
 
         def store_words(g, lo, hi):
             nc.sync.dma_start(out=words_out[g, :, lo:hi], in_=y_codes[g][:, lo:hi].bitcast(I32))
@@ -218,17 +286,25 @@ def tile_frozen_fp4_adapter_mix_g1_kernel(tc, x, w, u, mix, b, mag, act, out_0, 
             for q in range(4):
                 nc.sync.dma_start(out=scales_out[:, 4 * q : 4 * q + 4, :], in_=y_scales[32 * q : 32 * q + 16, :].bitcast(I32))
 
+        def load_mix(lo, hi):
+            nc.sync.dma_start(out=mix_rows[:, lo:hi], in_=mix[lo * P : hi * P, :].rearrange("(a p) e -> p a e", p=P))
+
+        def double_mix(lo, hi):
+            src = mix_rows[:, lo:hi].rearrange("p a e -> p (a e)").unsqueeze(2).to_broadcast([P, (hi - lo) * E, 2])
+            nc.scalar.copy(out=mix_twice[:, lo * E : hi * E], in_=src)
+
         make_identity(nc, ident[:])
-        load_w(0)
-        nc.sync.dma_start(out=mix_rows[:], in_=mix.rearrange("(a p) e -> p a e", p=P))
         nc.sync.dma_start(out=mag_rows[:], in_=mag.rearrange("(p c) -> p c", p=P))
-        load_x(0)
+        load_w(0)
+        load_mix(0, 2)
         load_u(0)
+        load_x(0)
         load_w(1)
+        load_act(0)
         load_w(2)
         load_w(3)
         load_x(1)
-        load_act(0)
+        load_mix(2, 2 * PAIRS)
         for pair in range(1, PAIRS):
             load_u(pair)
             load_x(2 * pair)
@@ -248,22 +324,21 @@ def tile_frozen_fp4_adapter_mix_g1_kernel(tc, x, w, u, mix, b, mag, act, out_0, 
                 turn_x(a, half)
                 empty_x(a, half)
 
+        spread_mag()
         share_w(0, V_HEAD)
-        nc.vector.tensor_copy(
-            out=mix_twice[:],
-            in_=mix_rows[:].rearrange("p a e -> p (a e)").unsqueeze(2).to_broadcast([P, 2 * PAIRS * E, 2]),
-        )
-        quantize_w(0)
+        double_mix(0, 2)
         weigh(0)
+        quantize_w(0)
         prepare_x(0)
         share_w(1, V_HEAD)
         quantize_x(0)
         quantize_w(1)
-        spread_mag()
+        make_gate(0, 1)
         share_w(2, V_HEAD)
-        quantize_w(2)
         share_w(3, V_HEAD)
+        quantize_w(2)
         quantize_w(3)
+        double_mix(2, 2 * PAIRS)
 
         for a in range(2 * PAIRS):
             j, i = divmod(a, 2)
@@ -273,9 +348,7 @@ def tile_frozen_fp4_adapter_mix_g1_kernel(tc, x, w, u, mix, b, mag, act, out_0, 
             if a + 1 < 2 * PAIRS:
                 prepare_x(a + 1)
             multiply(j, (i,))
-            if a == 0:
-                make_gate(0)
-            else:
+            if a > 0:
                 finish(*divmod(a - 1, 2))
             lo, hi = (V_FIRST, (V_FIRST + G) // 2) if i == 0 else ((V_FIRST + G) // 2, G)
             interleave_w(unit, "scalar", lo, hi)
@@ -286,37 +359,47 @@ def tile_frozen_fp4_adapter_mix_g1_kernel(tc, x, w, u, mix, b, mag, act, out_0, 
                     quantize_w(unit - 1)
             else:
                 interleave_w(unit, "vector", 0, V_FIRST)
-                make_gate(j + 1)
+                make_gate(j + 1, 1 if j + 1 < PAIRS or G_GATE else 2)
             if a + 1 < 2 * PAIRS:
                 quantize_x(a + 1)
-        load_act_chunk(2)
+        interleave_w(2 * PASSES, "vector", 0, V_8)
 
-        plan = {}
+        plan = {PAIRS - 2: [], PAIRS - 1: []}
         p = 0
-        for j in range(len(PLANES) + 1):
-            n = PLANES[j] if j < len(PLANES) else 0
-            plan[j] = list(range(p, p + n))
-            p = p + n
-        assert p == STEPS
+        for j in range(PAIRS, STEPS):
+            n = 0 if j < PLANE_START else (1 if j < DOUBLE_FROM else 2)
+            plan[j] = list(range(p, min(p + n, j - 1)))
+            p = p + len(plan[j])
+        assert p == STEPS - 2
         stored = 0
-        for j in range(PAIRS, len(PLANES) + 1):
+        for j in range(PAIRS, STEPS):
             unit = j + PASSES
             has_w = unit < CHUNKS * PASSES
             if unit + PASSES < CHUNKS * PASSES:
                 load_w(unit + PASSES)
+            if j == PAIRS:
+                load_act_chunk(2)
             if j == 2 * PAIRS:
                 load_act_chunk(3)
-            if unit - 1 < CHUNKS * PASSES:
+            if j == PAIRS:
                 quantize_w(unit - 1)
-            if j < STEPS:
+            elif j % 2 == 0 and unit - 2 < CHUNKS * PASSES:
+                quantize_w(unit - 2)
+            if G_GATE and j % 2 == 0 and j <= STEPS - PAIRS:
+                make_gate(j + 1, 1, nc.gpsimd)
+            if j < STEPS - 1:
                 multiply(j, (0, 1))
+            else:
+                multiply(j, (0,))
+                multiply(j, (1,))
             if j <= STEPS:
                 if j > PAIRS:
                     finish(j - 1, 0)
                 finish(j - 1, 1)
             todo = list(plan[j - 1])
             for q in plan[j]:
-                round_y(q)
+                if q not in G_CAST:
+                    round_y(q, "vector" if q in V_CAST else "scalar")
                 if todo:
                     empty_y(todo.pop(0))
             for q in todo:
@@ -324,21 +407,52 @@ def tile_frozen_fp4_adapter_mix_g1_kernel(tc, x, w, u, mix, b, mag, act, out_0, 
             for q in plan[j]:
                 turn_y(q)
             if has_w:
-                share_w(unit, V_MID)
-            if j + 1 < STEPS:
-                make_gate(j + 1)
-            for q in plan[j - 1]:
-                quantize_y(q)
+                if j == PAIRS:
+                    interleave_w(unit, "scalar", max(V_8, V_EVEN), G)
+                elif j % 2 == 0:
+                    interleave_w(unit, "scalar", V_EVEN, G)
+                else:
+                    share_w(unit, V_MID)
+                    interleave_w(unit - 1, "vector", V_8 if j == PAIRS + 1 else 0, V_EVEN)
+            if j % 2 == 1 and j + 1 < STEPS:
+                make_gate(j + 1, 1 if G_GATE else 2)
+            if G_GATE and j == STEPS - 2:
+                make_gate(j + 1, 1)
+            ready = plan[j - 2]
+            for q in ready:
+                if q >= STEPS - 2:
+                    quantize_y(q, 1)
+                elif q % 2 == 1:
+                    quantize_y(q - 1, 2)
             upto = min(STEPS, j, j - STORE_LAG + 1 + max(0, j - 2 * PAIRS))
             while stored < upto:
                 store_y(stored)
                 stored = stored + 1
-            for q in plan[j - 1]:
-                g, pair = divmod(q, PAIRS)
-                if g < CHUNKS - 1 and pair == PAIRS - 1:
-                    store_words(g, 0, M)
-                if g == CHUNKS - 1 and pair == PAIRS - 2:
-                    store_words(g, 0, M - 2 * P)
-                if g == CHUNKS - 1 and pair == PAIRS - 1:
-                    store_words(g, M - 2 * P, M)
-                    store_scales()
+            for q in ready:
+                if q % 2 == 1:
+                    store_words(q // PAIRS, (q - 1) % PAIRS * 2 * P, (q % PAIRS + 1) * 2 * P)
+
+        last = STEPS - 1
+        g = CHUNKS - 1
+        round_y(last - 1, "scalar")
+        finish(last, 0)
+        store_tile(0)
+        finish(last, 1)
+        store_tile(1)
+        for q in plan[last]:
+            empty_y(q)
+        turn_y(last - 1)
+        last_round(0)
+        last_round(1)
+        empty_y(last - 1)
+        last_empty(0)
+        last_empty(1)
+        for q in plan[last - 1] + plan[last]:
+            if q % 2 == 1:
+                quantize_y(q - 1, 2)
+                store_words(q // PAIRS, (q - 1) % PAIRS * 2 * P, (q % PAIRS + 1) * 2 * P)
+        quantize_y(last - 1, 1)
+        last_quantize(0)
+        last_quantize(1)
+        store_words(g, M // 2, M)
+        store_scales()

@@ -13,127 +13,124 @@ I32 = mybir.dt.int32
 U8 = mybir.dt.uint8
 FP8X4 = mybir.dt.float8_e4m3fn_x4
 MULT = mybir.AluOpType.mult
-ADD = mybir.AluOpType.add
 
 P = 128
 G = 512
-PASSES = 4
+PASSES = (K + E * R) // G
 CHUNKS = N // G
-PAIRS = M // (2 * P)
+TILES = M // P
+PAIRS = TILES // 2
 STEPS = CHUNKS * PAIRS
-V_HEAD = 320
-V_FIRST = 0
-V_MID = 320
-WIDE_FROM = 8
-SPLIT0 = 0
-G_COLS = 0
-V_EVEN = 0
-G_GATE = 1
-G_CAST = ()
-V_8 = 0
-Y_BUFS = 8
-PLANE_START = 6
-DOUBLE_FROM = 12
-V_CAST = (11, 13)
-STORE_LAG = 4
+SLABS = CHUNKS * PASSES
+LAST = STEPS - 1
+RUN = 4
+
+VECTOR_HALF = 256
+VECTOR_FIRST = 64
+VECTOR_LATER = 320
+GPSIMD_COLUMNS = 416
+PLANES_FROM = 6
+ACT_LEAD = 3
+SUM_BANKS = 6
 
 
 def tile_frozen_fp4_adapter_mix_g1_kernel(tc, x, w, u, mix, b, mag, act, out_0, out_1, out_2):
     nc = tc.nc
     with ExitStack() as ctx:
         sb = ctx.enter_context(tc.tile_pool(name="sb", bufs=1))
-        ps = ctx.enter_context(tc.psum_pool(name="ps", bufs=4))
+        ps = ctx.enter_context(tc.psum_pool(name="ps", bufs=1))
         ctx.enter_context(tc.manual_schedule())
 
         ident = sb.tile([P, P], F32, name="ident")
-        mag_rows = sb.tile([P, 16], BF16, name="mag_rows")
+        mag_rows = sb.tile([P, N // P], BF16, name="mag_rows")
         mag_all = sb.tile([P, N], BF16, name="mag_all")
-        mix_rows = sb.tile([P, 2 * PAIRS, E], BF16, name="mix_rows")
-        mix_twice = sb.tile([P, 2 * PAIRS * E, 2], BF16, name="mix_twice")
+        mix_rows = sb.tile([P, TILES, E], BF16, name="mix_rows")
+        mix_twice = sb.tile([P, TILES * E, 2], BF16, name="mix_twice")
         y_scales = sb.tile([P, M], U8, name="y_scales", align_bytes=64)
         words_out = out_1.rearrange("g p m t -> g p (m t)").bitcast(I32)
         scales_out = out_2.bitcast(I32)
 
-        x_raw, u_raw, h, act_sb, w_raw, w_side, w_mx, x_side, x_mx = {}, {}, {}, {}, {}, {}, {}, {}, {}
-        gate, acc, y, y_bf, y_bank, y_side, y_codes, x_bank = {}, {}, {}, {}, {}, {}, {}, {}
-        w_whole, act_two, y_whole = {}, {}, {}
+        x_raw, u_raw, h, act_sb, x_bank, x_side, x_mx = {}, {}, {}, {}, {}, {}, {}
+        w_raw, w_side, w_joint, w_mx = {}, {}, {}, {}
+        gate, total, y, y_bf, y_bank, y_side, y_codes = {}, {}, {}, {}, {}, {}, {}
 
-        def load_w(unit):
-            g, c = divmod(unit, PASSES)
+        def bank(k, shape):
+            return ps.tile(shape, F32, name="bank", tag="bank%d" % k)
+
+
+        def load_slab(s):
+            g, c = divmod(s, PASSES)
             rows = w[c * G : (c + 1) * G, :] if c < PASSES - 1 else b
-            t = sb.tile([P, 4, G], BF16, name="w_raw", bufs=6)
-            src = rows[:, g * G : (g + 1) * G].rearrange("(p j) n -> p j n", j=4)
-            if unit == 0 and SPLIT0:
-                nc.sync.dma_start(out=t[:, :, :SPLIT0], in_=src[:, :, :SPLIT0])
-                nc.sync.dma_start(out=t[:, :, SPLIT0:], in_=src[:, :, SPLIT0:])
-            else:
-                nc.sync.dma_start(out=t[:], in_=src)
-            w_raw[unit] = t
+            w_raw[s] = sb.tile([P, 4, G], BF16, name="w_raw", bufs=6)
+            nc.sync.dma_start(out=w_raw[s][:], in_=rows[:, g * G : (g + 1) * G].rearrange("(p t) n -> p t n", t=4))
 
         def load_x(a):
-            t = sb.tile([P, K], BF16, name="x_raw", bufs=5)
-            nc.sync.dma_start(out=t[:], in_=x[a * P : (a + 1) * P, :])
-            x_raw[a] = t
+            x_raw[a] = sb.tile([P, K], BF16, name="x_raw", bufs=4)
+            nc.sync.dma_start(out=x_raw[a][:], in_=x[a * P : (a + 1) * P, :])
 
         def load_u(pair):
-            t = sb.tile([P, 2, G], BF16, name="u_raw", bufs=3)
-            nc.sync.dma_start(out=t[:], in_=u[pair * 2 * P : (pair + 1) * 2 * P, :].rearrange("(a p) r -> p a r", p=P))
-            u_raw[pair] = t
+            u_raw[pair] = sb.tile([P, 2, G], BF16, name="u_raw", bufs=3)
+            rows = u[pair * 2 * P : (pair + 1) * 2 * P, :]
+            nc.sync.dma_start(out=u_raw[pair][:], in_=rows.rearrange("(a p) r -> p a r", p=P))
+
+        def load_mix(lo, hi):
+            nc.sync.dma_start(out=mix_rows[:, lo:hi], in_=mix[lo * P : hi * P, :].rearrange("(a p) e -> p a e", p=P))
+
+        def shared_tag(j):
+            return "shared%d" % (j // 2 % 3)
 
         def load_act(j):
             g, pair = divmod(j, PAIRS)
-            t = sb.tile([P, 2, G], BF16, name="act_first", bufs=4)
+            if j >= PAIRS and j % 2 == 0:
+                act_sb[j] = sb.tile([P, 2, G], BF16, name="act_even", tag=shared_tag(j))
+            else:
+                act_sb[j] = sb.tile([P, 2, G], BF16, name="act_other", bufs=4)
             rows = act[pair * 2 * P : (pair + 1) * 2 * P, g * G : (g + 1) * G]
-            nc.sync.dma_start(out=t[:], in_=rows.rearrange("(a p) n -> p a n", p=P))
-            act_sb[j] = t[:]
+            nc.sync.dma_start(out=act_sb[j][:], in_=rows.rearrange("(a p) n -> p a n", p=P))
 
-        def load_act_chunk(g):
-            t = sb.tile([P, 2 * PAIRS, G], BF16, name="act_chunk", bufs=2)
-            nc.sync.dma_start(out=t[:], in_=act[:, g * G : (g + 1) * G].rearrange("(a p) n -> p a n", p=P))
-            for pair in range(PAIRS):
-                act_sb[g * PAIRS + pair] = t[:, 2 * pair : 2 * pair + 2, :]
-                act_two[g * PAIRS + pair] = t[:, 2 * pair : min(2 * pair + 4, 2 * PAIRS), :]
 
-        def spread_mag():
-            pairs = mag_rows[:].bitcast(F32)
+        def turn_mag(k):
+            words = mag_rows[:].bitcast(F32)
+            t = bank(4 + k, [P, 4, P])
+            for i in range(4):
+                nc.tensor.transpose(t[:, i, :], words[:, 4 * k + i : 4 * k + i + 1].to_broadcast([P, P]), ident[:])
+            return t
+
+        def spread_mag(k, t):
             dst = mag_all[:].bitcast(F32).rearrange("q (p k i) -> q k p i", k=2, i=4)
-            for k in range(2):
-                bank = ps.tile([P, 4, P], F32, name="turn")
-                for i in range(4):
-                    col = 4 * k + i
-                    nc.tensor.transpose(bank[:, i, :], pairs[:, col : col + 1].to_broadcast([P, P]), ident[:])
-                nc.scalar.copy(out=dst[:, k], in_=bank[:].rearrange("q i p -> q p i"))
+            nc.scalar.copy(out=dst[:, k], in_=t[:].rearrange("q i p -> q p i"))
+
+        def double_mix(lo, hi):
+            src = mix_rows[:, lo:hi].rearrange("p a e -> p (a e)").unsqueeze(2).to_broadcast([P, (hi - lo) * E, 2])
+            nc.scalar.copy(out=mix_twice[:, lo * E : hi * E], in_=src)
+
 
         def weigh(pair):
-            t = sb.tile([P, 2 * G], BF16, name="h", bufs=2)
-            rows = slice(pair * 2 * E, (pair + 1) * 2 * E)
+            h[pair] = sb.tile([P, 2 * G], BF16, name="h", bufs=2)
+            weights = mix_twice[:, pair * 2 * E : (pair + 1) * 2 * E, :]
             nc.vector.tensor_tensor(
-                out=t[:].rearrange("p (e r i) -> p e r i", r=R // 2, i=2),
+                out=h[pair][:].rearrange("p (e r i) -> p e r i", r=R // 2, i=2),
                 in0=u_raw[pair][:].rearrange("p a (e r i) -> p (a e) r i", r=R // 2, i=2),
-                in1=mix_twice[:, rows, :].unsqueeze(2).to_broadcast([P, 2 * E, R // 2, 2]),
+                in1=weights.unsqueeze(2).to_broadcast([P, 2 * E, R // 2, 2]),
                 op=MULT,
             )
-            h[pair] = t
 
-        def interleave_w(unit, eng, lo, hi):
-            if unit not in w_side:
-                if unit < WIDE_FROM:
-                    t = sb.tile([P, G, 4], BF16, name="w_side", tag="side%d" % (unit % 3), align_bytes=64)
-                    w_side[unit] = t[:]
+        def lay_slab(s, copy, lo, hi):
+            if s not in w_side:
+                if s < 2 * PASSES:
+                    w_joint[s] = sb.tile([P, 1, G, 4], BF16, name="w_side", tag="side%d" % (s % 2), align_bytes=64)
                 else:
-                    t = sb.tile([P, 2, G, 4], BF16, name="w_side", tag="side%d" % ((unit // 2 + 1) % 3), align_bytes=64)
-                    w_side[unit], w_side[unit + 1] = t[:, 0], t[:, 1]
-                w_whole[unit] = t
-            if hi > lo:
-                dst = w_side[unit][:, lo:hi, :].rearrange("p (c i) t -> p c t i", i=4)
-                src = w_raw[unit][:, :, lo:hi].rearrange("p t (c i) -> p c t i", i=4)
-                if eng == "vector":
-                    nc.vector.tensor_copy(out=dst, in_=src)
-                elif eng == "scalar":
-                    nc.scalar.copy(out=dst, in_=src)
-                else:
-                    src = w_raw[unit][:, :, lo:hi].rearrange("p t n -> p n t")
-                    nc.gpsimd.tensor_scalar(out=w_side[unit][:, lo:hi, :], in0=src, scalar1=1.0, scalar2=0.0, op0=MULT, op1=ADD)
+                    w_joint[s] = sb.tile([P, 2, G, 4], BF16, name="w_side", tag="side%d" % (s // 2 % 2), align_bytes=64)
+                    w_side[s + 1] = w_joint[s][:, 1]
+                w_side[s] = w_joint[s][:, 0]
+            copy(
+                out=w_side[s][:, lo:hi, :].rearrange("p (c i) t -> p c t i", i=RUN),
+                in_=w_raw[s][:, :, lo:hi].rearrange("p t (c i) -> p c t i", i=RUN),
+            )
+
+        def share_slab(s, columns):
+            lay_slab(s, nc.scalar.copy, columns, G)
+            lay_slab(s, nc.vector.tensor_copy, 0, columns)
 
         def quantize(src, name, bufs, width):
             codes = sb.tile([P, width], U32, name=name + "_codes", bufs=bufs, align_bytes=64)
@@ -141,64 +138,62 @@ def tile_frozen_fp4_adapter_mix_g1_kernel(tc, x, w, u, mix, b, mag, act, out_0, 
             nc.vector.quantize_mx(out=codes[:].bitcast(FP8X4), scales=scales[:], in_=src)
             return codes, scales
 
-        def quantize_w(unit):
-            if unit < WIDE_FROM:
-                codes, scales = quantize(w_whole[unit][:].rearrange("p n t -> p (n t)"), "w", 8, G)
-                w_mx[unit] = codes[:], scales[:]
-            else:
-                codes, scales = quantize(w_whole[unit][:].rearrange("p c n t -> p (c n t)"), "w2", 4, 2 * G)
-                w_mx[unit] = codes[:, :G], scales[:, :G]
-                w_mx[unit + 1] = codes[:, G:], scales[:, G:]
+        def quantize_slabs(s):
+            n = 1 if s < 2 * PASSES else 2
+            src = w_joint[s][:].rearrange("p c n t -> p (c n t)")
+            codes, scales = quantize(src, "w%d" % n, 2 * PASSES // n, n * G)
+            for k in range(n):
+                w_mx[s + k] = codes[:, k * G : (k + 1) * G], scales[:, k * G : (k + 1) * G]
 
-        def turn_x(a, half):
-            bank = ps.tile([P, 2, 2, P], F32, name="turn")
-            for i in range(2):
-                c = 2 * half + i
-                if c < PASSES - 1:
-                    pairs = x_raw[a][:].bitcast(F32)[:, c * 256 : (c + 1) * 256]
-                else:
-                    pairs = h[a // 2][:].bitcast(F32)[:, (a % 2) * 256 : (a % 2 + 1) * 256]
-                for e in range(2):
-                    nc.tensor.transpose(bank[:, i, e, :], pairs[:, e::2], ident[:])
-            x_bank[a, half] = bank
-
-        def empty_x(a, half):
-            if half == 0:
-                x_side[a] = sb.tile([P, PASSES * P * 4], BF16, name="x_side", bufs=2, align_bytes=64)
+        def prepare_x(a):
+            x_side[a] = sb.tile([P, PASSES * P * 4], BF16, name="x_side", bufs=2, align_bytes=64)
             dst = x_side[a][:].bitcast(F32).rearrange("p (c r e) -> p c r e", c=PASSES, e=2)
-            nc.scalar.copy(out=dst[:, 2 * half : 2 * half + 2], in_=x_bank[a, half][:].rearrange("p c e r -> p c r e"))
+            for half in range(2):
+                t = bank(4 + (2 * a + half + 2) % 4, [P, 2, 2, P])
+                for i in range(2):
+                    c = 2 * half + i
+                    if c < PASSES - 1:
+                        words = x_raw[a][:].bitcast(F32)[:, c * G // 2 : (c + 1) * G // 2]
+                    else:
+                        words = h[a // 2][:].bitcast(F32)[:, a % 2 * G // 2 : (a % 2 + 1) * G // 2]
+                    for e in range(2):
+                        nc.tensor.transpose(t[:, i, e, :], words[:, e::2], ident[:])
+                nc.scalar.copy(out=dst[:, 2 * half : 2 * half + 2], in_=t[:].rearrange("p c e r -> p c r e"))
 
         def quantize_x(a):
-            x_mx[a] = quantize(x_side[a][:], "x", 2 * PAIRS, G)
+            x_mx[a] = quantize(x_side[a][:], "x", TILES, G)
 
-        def make_gate(j, n, eng=nc.vector):
+
+        def gate_columns(j, engine, lo, hi):
             g = j // PAIRS
-            if eng is nc.vector:
-                t = sb.tile([P, 2 * n, G], F32, name="gate", bufs=2)
-            else:
-                t = sb.tile([P, 2 * n, G], F32, name="gate_g", tag="side%d" % ((j + 3) // 2 % 3), align_bytes=64)
-            eng.tensor_tensor(
-                out=t[:],
-                in0=act_sb[j] if n == 1 else act_two[j],
-                in1=mag_all[:, g * G : (g + 1) * G].unsqueeze(1).to_broadcast([P, 2 * n, G]),
+            engine.tensor_tensor(
+                out=gate[j][:, :, lo:hi],
+                in0=act_sb[j][:, :, lo:hi],
+                in1=mag_all[:, g * G + lo : g * G + hi].unsqueeze(1).to_broadcast([P, 2, hi - lo]),
                 op=MULT,
             )
-            for k in range(n):
-                gate[j + k] = t[:, 2 * k : 2 * k + 2, :]
 
-        def multiply(j, tiles):
+        def make_gate(j):
+            gate[j] = sb.tile([P, 2, G], F32, name="gate", bufs=2)
+            gate_columns(j, nc.vector, 0, G)
+
+        def make_gate_gpsimd(j):
+            gate[j] = sb.tile([P, 2, G], F32, name="gate_odd", tag=shared_tag(j - 1))
+            gate_columns(j, nc.gpsimd, 0, GPSIMD_COLUMNS)
+
+        def multiply(j, tiles, passes):
             g, pair = divmod(j, PAIRS)
-            for i in tiles:
-                acc[j, i] = ps.tile([P, G], F32, name="acc")
-            for c in range(PASSES):
+            for c in passes:
                 w_codes, w_scales = w_mx[g * PASSES + c]
                 for i in tiles:
+                    if c == 0:
+                        n = 2 * j + i
+                        total[j, i] = bank(n % 4 if n < TILES else (n - TILES + 4) % SUM_BANKS, [P, G])
                     x_codes, x_scales = x_mx[2 * pair + i]
-                    cols = slice(c * P, (c + 1) * P)
                     nc.tensor.matmul_mx(
-                        out=acc[j, i][:],
-                        lhsT=x_codes[:, cols].bitcast(FP8X4),
-                        lhsT_scale=x_scales[:, cols],
+                        out=total[j, i][:],
+                        lhsT=x_codes[:, c * P : (c + 1) * P].bitcast(FP8X4),
+                        lhsT_scale=x_scales[:, c * P : (c + 1) * P],
                         rhs=w_codes.bitcast(FP8X4),
                         rhs_scale=w_scales,
                         start=(c == 0),
@@ -207,252 +202,208 @@ def tile_frozen_fp4_adapter_mix_g1_kernel(tc, x, w, u, mix, b, mag, act, out_0, 
 
         def finish(j, i):
             if i == 0:
-                y[j] = sb.tile([P, 2, G], F32, name="y", bufs=Y_BUFS)
-            nc.vector.tensor_tensor(out=y[j][:, i, :], in0=acc[j, i][:], in1=gate[j][:, i, :], op=MULT)
+                y[j] = sb.tile([P, 2, G], F32, name="y", bufs=10)
+            nc.vector.tensor_tensor(out=y[j][:, i, :], in0=total[j, i][:], in1=gate[j][:, i, :], op=MULT)
 
         def store_y(j):
             g, pair = divmod(j, PAIRS)
             rows = out_0[pair * 2 * P : (pair + 1) * 2 * P, g * G : (g + 1) * G]
             nc.sync.dma_start(out=rows.rearrange("(a p) n -> p a n", p=P), in_=y[j][:])
 
-        def store_tile(i):
-            a = 2 * PAIRS - 2 + i
-            nc.sync.dma_start(out=out_0[a * P : (a + 1) * P, N - G :], in_=y[STEPS - 1][:, i, :])
 
-        def round_y(j, eng):
-            if eng == "gpsimd":
-                t = sb.tile([P, 2, 2 * P, 2], BF16, name="y_bf_g", tag="side0", align_bytes=64)
-            else:
-                t = sb.tile([P, 2, 2 * P, 2], BF16, name="y_bf", bufs=3)
-            src = y[j][:].rearrange("q a (p e i) -> q e (a p) i", e=2, i=2)
-            if eng == "vector":
-                nc.vector.tensor_copy(out=t[:], in_=src)
-            elif eng == "scalar":
-                nc.scalar.copy(out=t[:], in_=src)
-            else:
-                nc.gpsimd.tensor_scalar(out=t[:], in0=src, scalar1=1.0, scalar2=0.0, op0=MULT, op1=ADD)
-            y_bf[j] = t
+        def round_y(src, tiles, copy):
+            t = sb.tile([P, 2, tiles * P, 2], BF16, name="y_bf", bufs=4)
+            copy(
+                out=t[:].rearrange("q e (r s) i -> q r e s i", s=RUN),
+                in_=src.rearrange("q (r s e i) -> q r e s i", s=RUN, e=2, i=2),
+            )
+            return t
 
-        def turn_y(j):
-            bank = ps.tile([P, 2, 2, P], F32, name="turn")
-            pairs = y_bf[j][:].rearrange("q e r i -> q (e r i)").bitcast(F32)
-            for a in range(2):
+        def turn_y(rounded, tiles, k):
+            t = bank(k, [P, tiles, 2, P])
+            words = rounded[:].rearrange("q e r i -> q (e r i)").bitcast(F32)
+            for a in range(tiles):
                 for e in range(2):
-                    s = (2 * e + a) * P
-                    nc.tensor.transpose(bank[:, a, e, :], pairs[:, s : s + P], ident[:])
-            y_bank[j] = bank
+                    first = (tiles * e + a) * P
+                    nc.tensor.transpose(t[:, a, e, :], words[:, first : first + P], ident[:])
+            return t
 
-        def empty_y(j):
-            if j % 2 == 0:
-                y_whole[j] = sb.tile([P, 2, 2 * P * 4], BF16, name="y_side", bufs=3, align_bytes=64)
-            t = y_whole[j - j % 2][:, j % 2, :]
-            dst = t.bitcast(F32).rearrange("p (a r e) -> p a r e", a=2, e=2)
-            nc.scalar.copy(out=dst, in_=y_bank[j][:].rearrange("p a e r -> p a r e"))
+        def empty_y(t, j, first, tiles):
+            if j not in y_side:
+                y_side[j] = sb.tile([P, 4 * P * 4], BF16, name="y_side", bufs=3, align_bytes=64)
+            dst = y_side[j][:, first * P * 4 : (first + tiles) * P * 4].bitcast(F32)
+            nc.scalar.copy(out=dst.rearrange("p (a r e) -> p a r e", a=tiles, e=2), in_=t[:].rearrange("p a e r -> p a r e"))
 
-        def quantize_y(j, n):
+        def quantize_y(j, first, tiles):
             g, pair = divmod(j, PAIRS)
-            if pair == 0:
+            if g not in y_codes:
                 y_codes[g] = sb.tile([P, M], U32, name="y_codes", bufs=2, align_bytes=64)
-            cols = slice(pair * 2 * P, (pair + n) * 2 * P)
-            src = y_whole[j - j % 2][:, j % 2 : j % 2 + n, :].rearrange("p k v -> p (k v)")
+            cols = slice((2 * pair + first) * P, (2 * pair + first + tiles) * P)
+            src = y_side[j][:, first * P * 4 : (first + tiles) * P * 4]
             nc.vector.quantize_mx(out=y_codes[g][:, cols].bitcast(FP8X4), scales=y_scales[4 * g :, cols], in_=src)
 
-        def last_round(i):
-            j = STEPS - 1
-            t = sb.tile([P, 2, P, 2], BF16, name="y_last", tag="y_bf", bufs=3)
-            nc.vector.tensor_copy(out=t[:], in_=y[j][:, i, :].rearrange("q (p e i) -> q e p i", e=2, i=2))
-            bank = ps.tile([P, 2, P], F32, name="turn")
-            pairs = t[:].rearrange("q e r i -> q (e r i)").bitcast(F32)
-            for e in range(2):
-                nc.tensor.transpose(bank[:, e, :], pairs[:, e * P : (e + 1) * P], ident[:])
-            y_bank[j, i] = bank
+        def round_step(j):
+            copy = nc.vector.tensor_copy if j >= LAST - 2 else nc.scalar.copy
+            y_bf[j] = round_y(y[j][:].rearrange("q a n -> q (a n)"), 2, copy)
 
-        def last_empty(i):
-            j = STEPS - 1
-            dst = y_whole[j - 1][:, 1, i * 4 * P : (i + 1) * 4 * P].bitcast(F32).rearrange("p (r e) -> p r e", e=2)
-            nc.scalar.copy(out=dst, in_=y_bank[j, i][:].rearrange("p e r -> p r e"))
+        def turn_step(j):
+            y_bank[j] = turn_y(y_bf[j], 2, SUM_BANKS + j % 2)
 
-        def last_quantize(i):
-            j = STEPS - 1
-            cols = slice(M - (2 - i) * P, M - (1 - i) * P)
-            src = y_whole[j - 1][:, 1, i * 4 * P : (i + 1) * 4 * P]
-            g = CHUNKS - 1
-            nc.vector.quantize_mx(out=y_codes[g][:, cols].bitcast(FP8X4), scales=y_scales[4 * g :, cols], in_=src)
+        def empty_step(j):
+            empty_y(y_bank[j], j - j % 2, 2 * (j % 2), 2)
 
-        def store_words(g, lo, hi):
-            nc.sync.dma_start(out=words_out[g, :, lo:hi], in_=y_codes[g][:, lo:hi].bitcast(I32))
+        def store_words(j):
+            g, pair = divmod(j, PAIRS)
+            cols = slice(pair * 2 * P, (pair + 2) * 2 * P)
+            nc.sync.dma_start(out=words_out[g, :, cols], in_=y_codes[g][:, cols].bitcast(I32))
 
-        def store_scales():
+        def store_scales(g):
             for q in range(4):
-                nc.sync.dma_start(out=scales_out[:, 4 * q : 4 * q + 4, :], in_=y_scales[32 * q : 32 * q + 16, :].bitcast(I32))
-
-        def load_mix(lo, hi):
-            nc.sync.dma_start(out=mix_rows[:, lo:hi], in_=mix[lo * P : hi * P, :].rearrange("(a p) e -> p a e", p=P))
-
-        def double_mix(lo, hi):
-            src = mix_rows[:, lo:hi].rearrange("p a e -> p (a e)").unsqueeze(2).to_broadcast([P, (hi - lo) * E, 2])
-            nc.scalar.copy(out=mix_twice[:, lo * E : hi * E], in_=src)
+                rows = slice(32 * q + 4 * g, 32 * q + 4 * g + 8)
+                nc.sync.dma_start(out=scales_out[g : g + 2, 4 * q : 4 * q + 4, :], in_=y_scales[rows, :].bitcast(I32))
 
         make_identity(nc, ident[:])
         nc.sync.dma_start(out=mag_rows[:], in_=mag.rearrange("(p c) -> p c", p=P))
-        load_w(0)
+        load_slab(0)
         load_mix(0, 2)
         load_u(0)
         load_x(0)
-        load_w(1)
         load_act(0)
-        load_w(2)
-        load_w(3)
+        for s in range(1, PASSES):
+            load_slab(s)
         load_x(1)
-        load_mix(2, 2 * PAIRS)
+        load_mix(2, TILES)
         for pair in range(1, PAIRS):
             load_u(pair)
             load_x(2 * pair)
-            load_w(PASSES + pair - 1)
+            load_slab(PASSES + pair - 1)
             load_x(2 * pair + 1)
             load_act(pair)
-        load_w(2 * PASSES - 1)
-        load_w(2 * PASSES)
-        load_act_chunk(1)
+        load_slab(2 * PASSES - 1)
+        load_act(PAIRS)
+        load_act(PAIRS + 1)
+        load_slab(2 * PASSES)
+        load_act(PAIRS + 2)
 
-        def share_w(unit, cols):
-            interleave_w(unit, "scalar", cols, G)
-            interleave_w(unit, "vector", 0, cols)
-
-        def prepare_x(a):
-            for half in range(2):
-                turn_x(a, half)
-                empty_x(a, half)
-
-        spread_mag()
-        share_w(0, V_HEAD)
+        mag_banks = [turn_mag(k) for k in range(2)]
+        share_slab(0, VECTOR_HALF)
         double_mix(0, 2)
+        for k in range(2):
+            spread_mag(k, mag_banks[k])
         weigh(0)
-        quantize_w(0)
+        quantize_slabs(0)
         prepare_x(0)
-        share_w(1, V_HEAD)
+        make_gate(0)
+        share_slab(1, VECTOR_HALF)
         quantize_x(0)
-        quantize_w(1)
-        make_gate(0, 1)
-        share_w(2, V_HEAD)
-        share_w(3, V_HEAD)
-        quantize_w(2)
-        quantize_w(3)
-        double_mix(2, 2 * PAIRS)
+        quantize_slabs(1)
+        multiply(0, [0], range(2))
+        share_slab(2, VECTOR_HALF)
+        share_slab(3, VECTOR_HALF)
+        quantize_slabs(2)
+        quantize_slabs(3)
+        double_mix(2, TILES)
 
-        for a in range(2 * PAIRS):
+        for a in range(TILES):
             j, i = divmod(a, 2)
-            unit = PASSES + j
+            s = PASSES + j
+            share = VECTOR_FIRST if j + 1 < PAIRS else VECTOR_HALF
+            middle = (share + G) // 2
             if i == 1 and j > 0:
-                load_w(unit + PASSES)
-            if a + 1 < 2 * PAIRS:
+                load_slab(s + PASSES)
+            if a + 1 < TILES:
                 prepare_x(a + 1)
-            multiply(j, (i,))
-            if a > 0:
-                finish(*divmod(a - 1, 2))
-            lo, hi = (V_FIRST, (V_FIRST + G) // 2) if i == 0 else ((V_FIRST + G) // 2, G)
-            interleave_w(unit, "scalar", lo, hi)
+            multiply(j, [i], range(2 if a == 0 else 0, PASSES))
+            if 0 < a < TILES - 1:
+                finish((a - 1) // 2, (a - 1) % 2)
             if i == 0:
+                lay_slab(s, nc.scalar.copy, share, middle)
                 if j + 1 < PAIRS:
                     weigh(j + 1)
                 if j > 0:
-                    quantize_w(unit - 1)
+                    quantize_slabs(s - 1)
             else:
-                interleave_w(unit, "vector", 0, V_FIRST)
-                make_gate(j + 1, 1 if j + 1 < PAIRS or G_GATE else 2)
-            if a + 1 < 2 * PAIRS:
+                lay_slab(s, nc.scalar.copy, middle, G)
+                lay_slab(s, nc.vector.tensor_copy, 0, share)
+                if j + 1 == PAIRS:
+                    quantize_slabs(s)
+                make_gate(j + 1)
+            if a + 1 < TILES:
                 quantize_x(a + 1)
-        interleave_w(2 * PASSES, "vector", 0, V_8)
 
-        plan = {PAIRS - 2: [], PAIRS - 1: []}
-        p = 0
-        for j in range(PAIRS, STEPS):
-            n = 0 if j < PLANE_START else (1 if j < DOUBLE_FROM else 2)
-            plan[j] = list(range(p, min(p + n, j - 1)))
-            p = p + len(plan[j])
-        assert p == STEPS - 2
+        rounded_at = {j: [] for j in range(STEPS)}
+        done = 0
+        for j in range(PLANES_FROM, STEPS):
+            if j % 2 == 0 or j >= STEPS - PAIRS:
+                rounded_at[j] = [done, done + 1]
+                done = done + 2
+
         stored = 0
         for j in range(PAIRS, STEPS):
-            unit = j + PASSES
-            has_w = unit < CHUNKS * PASSES
-            if unit + PASSES < CHUNKS * PASSES:
-                load_w(unit + PASSES)
-            if j == PAIRS:
-                load_act_chunk(2)
-            if j == 2 * PAIRS:
-                load_act_chunk(3)
-            if j == PAIRS:
-                quantize_w(unit - 1)
-            elif j % 2 == 0 and unit - 2 < CHUNKS * PASSES:
-                quantize_w(unit - 2)
-            if G_GATE and j % 2 == 0 and j <= STEPS - PAIRS:
-                make_gate(j + 1, 1, nc.gpsimd)
-            if j < STEPS - 1:
-                multiply(j, (0, 1))
+            s = j + PASSES
+            if j + ACT_LEAD < STEPS:
+                load_act(j + ACT_LEAD)
+            if s + PASSES < SLABS:
+                load_slab(s + PASSES)
+            if j % 2 == 0:
+                make_gate_gpsimd(j + 1)
+            if j < LAST:
+                multiply(j, [0, 1], range(PASSES // 2))
             else:
-                multiply(j, (0,))
-                multiply(j, (1,))
-            if j <= STEPS:
-                if j > PAIRS:
-                    finish(j - 1, 0)
-                finish(j - 1, 1)
-            todo = list(plan[j - 1])
-            for q in plan[j]:
-                if q not in G_CAST:
-                    round_y(q, "vector" if q in V_CAST else "scalar")
-                if todo:
-                    empty_y(todo.pop(0))
-            for q in todo:
-                empty_y(q)
-            for q in plan[j]:
-                turn_y(q)
-            if has_w:
-                if j == PAIRS:
-                    interleave_w(unit, "scalar", max(V_8, V_EVEN), G)
-                elif j % 2 == 0:
-                    interleave_w(unit, "scalar", V_EVEN, G)
+                multiply(j, [0], range(PASSES))
+            for q in rounded_at[j - 1]:
+                turn_step(q)
+            if j < LAST:
+                multiply(j, [0, 1], range(PASSES // 2, PASSES))
+            else:
+                multiply(j, [1], range(PASSES))
+            finish(j - 1, 0)
+            finish(j - 1, 1)
+            for q in rounded_at[j]:
+                round_step(q)
+            if s < SLABS:
+                if j % 2 == 0:
+                    lay_slab(s, nc.scalar.copy, 0, G)
                 else:
-                    share_w(unit, V_MID)
-                    interleave_w(unit - 1, "vector", V_8 if j == PAIRS + 1 else 0, V_EVEN)
-            if j % 2 == 1 and j + 1 < STEPS:
-                make_gate(j + 1, 1 if G_GATE else 2)
-            if G_GATE and j == STEPS - 2:
-                make_gate(j + 1, 1)
-            ready = plan[j - 2]
-            for q in ready:
-                if q >= STEPS - 2:
-                    quantize_y(q, 1)
-                elif q % 2 == 1:
-                    quantize_y(q - 1, 2)
-            upto = min(STEPS, j, j - STORE_LAG + 1 + max(0, j - 2 * PAIRS))
-            while stored < upto:
+                    share_slab(s, VECTOR_LATER)
+            for q in rounded_at[j - 1]:
+                empty_step(q)
+            ready = []
+            if j % 2 == 1:
+                gate_columns(j, nc.vector, GPSIMD_COLUMNS, G)
+                if s < SLABS:
+                    quantize_slabs(s - 1)
+                ready = rounded_at[j - 3][:1] + rounded_at[j - 2][:1]
+                for q in ready:
+                    quantize_y(q, 0, 4)
+                if j < LAST:
+                    make_gate(j + 1)
+            while stored < min(j, j - PAIRS + 1 + max(0, j - 2 * PAIRS)):
                 store_y(stored)
                 stored = stored + 1
             for q in ready:
-                if q % 2 == 1:
-                    store_words(q // PAIRS, (q - 1) % PAIRS * 2 * P, (q % PAIRS + 1) * 2 * P)
+                store_words(q)
+                if q == 2 * PAIRS - 2:
+                    store_scales(0)
 
-        last = STEPS - 1
-        g = CHUNKS - 1
-        round_y(last - 1, "scalar")
-        finish(last, 0)
-        store_tile(0)
-        finish(last, 1)
-        store_tile(1)
-        for q in plan[last]:
-            empty_y(q)
-        turn_y(last - 1)
-        last_round(0)
-        last_round(1)
-        empty_y(last - 1)
-        last_empty(0)
-        last_empty(1)
-        for q in plan[last - 1] + plan[last]:
-            if q % 2 == 1:
-                quantize_y(q - 1, 2)
-                store_words(q // PAIRS, (q - 1) % PAIRS * 2 * P, (q % PAIRS + 1) * 2 * P)
-        quantize_y(last - 1, 1)
-        last_quantize(0)
-        last_quantize(1)
-        store_words(g, M // 2, M)
-        store_scales()
+        round_step(LAST - 1)
+        for i in range(2):
+            finish(LAST, i)
+            a = TILES - 2 + i
+            nc.sync.dma_start(out=out_0[a * P : (a + 1) * P, N - G :], in_=y[LAST][:, i, :])
+        for q in rounded_at[LAST]:
+            turn_step(q)
+            empty_step(q)
+        turn_step(LAST - 1)
+        last_banks = [turn_y(round_y(y[LAST][:, i, :], 1, nc.vector.tensor_copy), 1, i) for i in range(2)]
+        empty_step(LAST - 1)
+        for i in range(2):
+            empty_y(last_banks[i], LAST - 1, 2 + i, 1)
+        for q in rounded_at[LAST - 1][:1] + rounded_at[LAST][:1]:
+            quantize_y(q, 0, 4)
+            store_words(q)
+        quantize_y(LAST - 1, 0, 2)
+        for i in range(2):
+            quantize_y(LAST - 1, 2 + i, 1)
+        store_words(LAST - 1)
+        store_scales(2)

@@ -30,7 +30,7 @@ VECTOR_FIRST = 64
 VECTOR_LATER = 320
 GPSIMD_COLUMNS = 416
 PLANES_FROM = 6
-ACT_LEAD = 3
+ACT_LEAD_EVEN, ACT_LEAD_ODD = 3, 5
 SUM_BANKS = 6
 
 
@@ -46,13 +46,12 @@ def tile_frozen_fp4_adapter_mix_g1_kernel(tc, x, w, u, mix, b, mag, act, out_0, 
         mag_all = sb.tile([P, N], BF16, name="mag_all")
         mix_rows = sb.tile([P, TILES, E], BF16, name="mix_rows")
         mix_twice = sb.tile([P, TILES * E, 2], BF16, name="mix_twice")
-        y_scales = sb.tile([P, M], U8, name="y_scales", align_bytes=64)
         words_out = out_1.rearrange("g p m t -> g p (m t)").bitcast(I32)
         scales_out = out_2.bitcast(I32)
 
         x_raw, u_raw, h, act_sb, x_bank, x_side, x_mx = {}, {}, {}, {}, {}, {}, {}
         w_raw, w_side, w_joint, w_mx = {}, {}, {}, {}
-        gate, total, y, y_bf, y_bank, y_side, y_codes = {}, {}, {}, {}, {}, {}, {}
+        gate, total, y, y_bf, y_bank, y_side, y_codes, y_scales = {}, {}, {}, {}, {}, {}, {}, {}
 
         def bank(k, shape):
             return ps.tile(shape, F32, name="bank", tag="bank%d" % k)
@@ -238,9 +237,11 @@ def tile_frozen_fp4_adapter_mix_g1_kernel(tc, x, w, u, mix, b, mag, act, out_0, 
             g, pair = divmod(j, PAIRS)
             if g not in y_codes:
                 y_codes[g] = sb.tile([P, M], U32, name="y_codes", bufs=2, align_bytes=64)
+                if g % 2 == 0:
+                    y_scales[g] = sb.tile([P, M], U8, name="y_scales", bufs=2, align_bytes=64)
             cols = slice((2 * pair + first) * P, (2 * pair + first + tiles) * P)
             src = y_side[j][:, first * P * 4 : (first + tiles) * P * 4]
-            nc.vector.quantize_mx(out=y_codes[g][:, cols].bitcast(FP8X4), scales=y_scales[4 * g :, cols], in_=src)
+            nc.vector.quantize_mx(out=y_codes[g][:, cols].bitcast(FP8X4), scales=y_scales[g - g % 2][4 * (g % 2) :, cols], in_=src)
 
         def round_step(j):
             copy = nc.vector.tensor_copy if j >= LAST - 2 else nc.scalar.copy
@@ -252,15 +253,15 @@ def tile_frozen_fp4_adapter_mix_g1_kernel(tc, x, w, u, mix, b, mag, act, out_0, 
         def empty_step(j):
             empty_y(y_bank[j], j - j % 2, 2 * (j % 2), 2)
 
-        def store_words(j):
+        def store_words(j, steps):
             g, pair = divmod(j, PAIRS)
-            cols = slice(pair * 2 * P, (pair + 2) * 2 * P)
+            cols = slice(pair * 2 * P, (pair + steps) * 2 * P)
             nc.sync.dma_start(out=words_out[g, :, cols], in_=y_codes[g][:, cols].bitcast(I32))
 
         def store_scales(g):
             for q in range(4):
-                rows = slice(32 * q + 4 * g, 32 * q + 4 * g + 8)
-                nc.sync.dma_start(out=scales_out[g : g + 2, 4 * q : 4 * q + 4, :], in_=y_scales[rows, :].bitcast(I32))
+                src = y_scales[g][32 * q : 32 * q + 8, :].bitcast(I32)
+                nc.sync.dma_start(out=scales_out[g : g + 2, 4 * q : 4 * q + 4, :], in_=src)
 
         make_identity(nc, ident[:])
         nc.sync.dma_start(out=mag_rows[:], in_=mag.rearrange("(p c) -> p c", p=P))
@@ -284,6 +285,7 @@ def tile_frozen_fp4_adapter_mix_g1_kernel(tc, x, w, u, mix, b, mag, act, out_0, 
         load_act(PAIRS + 1)
         load_slab(2 * PASSES)
         load_act(PAIRS + 2)
+        load_act(PAIRS + 3)
 
         mag_banks = [turn_mag(k) for k in range(2)]
         share_slab(0, VECTOR_HALF)
@@ -304,32 +306,39 @@ def tile_frozen_fp4_adapter_mix_g1_kernel(tc, x, w, u, mix, b, mag, act, out_0, 
         quantize_slabs(3)
         double_mix(2, TILES)
 
+        def lay_half(n):
+            s = PASSES + n // 2
+            share = VECTOR_FIRST if s + 1 < 2 * PASSES else VECTOR_HALF
+            middle = (share + G) // 2
+            if n % 2 == 0:
+                lay_slab(s, nc.scalar.copy, share, middle)
+            else:
+                lay_slab(s, nc.scalar.copy, middle, G)
+                lay_slab(s, nc.vector.tensor_copy, 0, share)
+
         for a in range(TILES):
             j, i = divmod(a, 2)
-            s = PASSES + j
-            share = VECTOR_FIRST if j + 1 < PAIRS else VECTOR_HALF
-            middle = (share + G) // 2
             if i == 1 and j > 0:
-                load_slab(s + PASSES)
+                load_slab(2 * PASSES + j)
             if a + 1 < TILES:
                 prepare_x(a + 1)
             multiply(j, [i], range(2 if a == 0 else 0, PASSES))
             if 0 < a < TILES - 1:
                 finish((a - 1) // 2, (a - 1) % 2)
             if i == 0:
-                lay_slab(s, nc.scalar.copy, share, middle)
                 if j + 1 < PAIRS:
                     weigh(j + 1)
                 if j > 0:
-                    quantize_slabs(s - 1)
-            else:
-                lay_slab(s, nc.scalar.copy, middle, G)
-                lay_slab(s, nc.vector.tensor_copy, 0, share)
-                if j + 1 == PAIRS:
-                    quantize_slabs(s)
-                make_gate(j + 1)
+                    make_gate(j)
+            elif j > 0:
+                quantize_slabs(PASSES + j - 1)
             if a + 1 < TILES:
                 quantize_x(a + 1)
+            if a > 0:
+                lay_half(a - 1)
+        lay_half(TILES - 1)
+        quantize_slabs(2 * PASSES - 1)
+        make_gate(PAIRS)
 
         rounded_at = {j: [] for j in range(STEPS)}
         done = 0
@@ -341,22 +350,26 @@ def tile_frozen_fp4_adapter_mix_g1_kernel(tc, x, w, u, mix, b, mag, act, out_0, 
         stored = 0
         for j in range(PAIRS, STEPS):
             s = j + PASSES
-            if j + ACT_LEAD < STEPS:
-                load_act(j + ACT_LEAD)
+            ahead = j + (ACT_LEAD_ODD if j % 2 == 0 else ACT_LEAD_EVEN)
+            if ahead < STEPS:
+                load_act(ahead)
             if s + PASSES < SLABS:
                 load_slab(s + PASSES)
             if j % 2 == 0:
                 make_gate_gpsimd(j + 1)
-            if j < LAST:
-                multiply(j, [0, 1], range(PASSES // 2))
-            else:
+            early, late = range(PASSES // 2), range(PASSES // 2, PASSES)
+            if j == LAST:
                 multiply(j, [0], range(PASSES))
+            elif j % PAIRS != 1:
+                multiply(j, [0, 1], early)
             for q in rounded_at[j - 1]:
                 turn_step(q)
-            if j < LAST:
-                multiply(j, [0, 1], range(PASSES // 2, PASSES))
-            else:
+            if j % PAIRS == 0:
+                multiply(j + 1, [0, 1], early)
+            if j == LAST:
                 multiply(j, [1], range(PASSES))
+            else:
+                multiply(j, [0, 1], late)
             finish(j - 1, 0)
             finish(j - 1, 1)
             for q in rounded_at[j]:
@@ -382,7 +395,7 @@ def tile_frozen_fp4_adapter_mix_g1_kernel(tc, x, w, u, mix, b, mag, act, out_0, 
                 store_y(stored)
                 stored = stored + 1
             for q in ready:
-                store_words(q)
+                store_words(q, 2)
                 if q == 2 * PAIRS - 2:
                     store_scales(0)
 
@@ -401,9 +414,10 @@ def tile_frozen_fp4_adapter_mix_g1_kernel(tc, x, w, u, mix, b, mag, act, out_0, 
             empty_y(last_banks[i], LAST - 1, 2 + i, 1)
         for q in rounded_at[LAST - 1][:1] + rounded_at[LAST][:1]:
             quantize_y(q, 0, 4)
-            store_words(q)
+            store_words(q, 2)
         quantize_y(LAST - 1, 0, 2)
+        store_words(LAST - 1, 1)
         for i in range(2):
             quantize_y(LAST - 1, 2 + i, 1)
-        store_words(LAST - 1)
+        store_words(LAST, 1)
         store_scales(2)

@@ -27,7 +27,7 @@ RUN = 4
 
 VECTOR_HALF = 256
 VECTOR_FIRST = 64
-VECTOR_LATER = 320
+VECTOR_LATER = 352
 GPSIMD_COLUMNS = 416
 PLANES_FROM = 6
 ACT_LEAD_EVEN, ACT_LEAD_ODD = 3, 5
@@ -44,36 +44,49 @@ def tile_frozen_fp4_adapter_mix_g1_kernel(tc, x, w, u, mix, b, mag, act, out_0, 
         ident = sb.tile([P, P], F32, name="ident")
         mag_rows = sb.tile([P, N // P], BF16, name="mag_rows")
         mag_all = sb.tile([P, N], BF16, name="mag_all")
-        mix_rows = sb.tile([P, TILES, E], BF16, name="mix_rows")
+        mix_rows = sb.tile([P, PAIRS, 2 * E], BF16, name="mix_rows")
         mix_twice = sb.tile([P, TILES * E, 2], BF16, name="mix_twice")
         words_out = out_1.rearrange("g p m t -> g p (m t)").bitcast(I32)
         scales_out = out_2.bitcast(I32)
 
-        x_raw, u_raw, h, act_sb, x_bank, x_side, x_mx = {}, {}, {}, {}, {}, {}, {}
-        w_raw, w_side, w_joint, w_mx = {}, {}, {}, {}
+        xu_raw, h, act_sb, x_side, x_mx = {}, {}, {}, {}, {}
+        w_raw, w_side, w_joint, w_two, w_mx = {}, {}, {}, {}, {}
         gate, total, y, y_bf, y_bank, y_side, y_codes, y_scales = {}, {}, {}, {}, {}, {}, {}, {}
 
         def bank(k, shape):
             return ps.tile(shape, F32, name="bank", tag="bank%d" % k)
 
 
+        def pair_rows(t, pair):
+            return t[pair * 2 * P : (pair + 1) * 2 * P, :].rearrange("(p i) n -> p i n", i=2)
+
+        def pass_rows(c):
+            rows = w[c * G : (c + 1) * G, :] if c < PASSES - 1 else b
+            return rows.rearrange("(p t) n -> p t n", t=4)
+
         def load_slab(s):
             g, c = divmod(s, PASSES)
-            rows = w[c * G : (c + 1) * G, :] if c < PASSES - 1 else b
-            w_raw[s] = sb.tile([P, 4, G], BF16, name="w_raw", bufs=6)
-            nc.sync.dma_start(out=w_raw[s][:], in_=rows[:, g * G : (g + 1) * G].rearrange("(p t) n -> p t n", t=4))
+            t = sb.tile([P, 4, G], BF16, name="w_raw", bufs=4)
+            nc.sync.dma_start(out=t[:], in_=pass_rows(c)[:, :, g * G : (g + 1) * G])
+            w_raw[s] = t[:]
 
-        def load_x(a):
-            x_raw[a] = sb.tile([P, K], BF16, name="x_raw", bufs=4)
-            nc.sync.dma_start(out=x_raw[a][:], in_=x[a * P : (a + 1) * P, :])
+        def load_two_slabs(c):
+            t = sb.tile([P, 4, 2 * G], BF16, name="w_wide", tag="wide%d" % c)
+            nc.sync.dma_start(out=t[:], in_=pass_rows(c)[:, :, 2 * G :])
+            w_raw[2 * PASSES + c], w_raw[3 * PASSES + c] = t[:, :, :G], t[:, :, G:]
 
         def load_u(pair):
-            u_raw[pair] = sb.tile([P, 2, G], BF16, name="u_raw", bufs=3)
-            rows = u[pair * 2 * P : (pair + 1) * 2 * P, :]
-            nc.sync.dma_start(out=u_raw[pair][:], in_=rows.rearrange("(a p) r -> p a r", p=P))
+            xu_raw[pair] = sb.tile([P, 2 * (K + G)], BF16, name="xu_raw", tag="wide%d" % pair)
+            dst = xu_raw[pair][:, 2 * K :].rearrange("p (i r) -> p i r", i=2)
+            nc.sync.dma_start(out=dst, in_=pair_rows(u, pair))
+
+        def load_x(a):
+            pair, i = divmod(a, 2)
+            nc.sync.dma_start(out=xu_raw[pair][:, i * K : (i + 1) * K], in_=pair_rows(x, pair)[:, i, :])
 
         def load_mix(lo, hi):
-            nc.sync.dma_start(out=mix_rows[:, lo:hi], in_=mix[lo * P : hi * P, :].rearrange("(a p) e -> p a e", p=P))
+            src = mix[lo * 2 * P : hi * 2 * P, :].rearrange("(c p i) e -> p c (i e)", p=P, i=2)
+            nc.sync.dma_start(out=mix_rows[:, lo:hi], in_=src)
 
         def shared_tag(j):
             return "shared%d" % (j // 2 % 3)
@@ -84,8 +97,7 @@ def tile_frozen_fp4_adapter_mix_g1_kernel(tc, x, w, u, mix, b, mag, act, out_0, 
                 act_sb[j] = sb.tile([P, 2, G], BF16, name="act_even", tag=shared_tag(j))
             else:
                 act_sb[j] = sb.tile([P, 2, G], BF16, name="act_other", bufs=4)
-            rows = act[pair * 2 * P : (pair + 1) * 2 * P, g * G : (g + 1) * G]
-            nc.sync.dma_start(out=act_sb[j][:], in_=rows.rearrange("(a p) n -> p a n", p=P))
+            nc.sync.dma_start(out=act_sb[j][:], in_=pair_rows(act, pair)[:, :, g * G : (g + 1) * G])
 
 
         def turn_mag(k):
@@ -100,8 +112,8 @@ def tile_frozen_fp4_adapter_mix_g1_kernel(tc, x, w, u, mix, b, mag, act, out_0, 
             nc.scalar.copy(out=dst[:, k], in_=t[:].rearrange("q i p -> q p i"))
 
         def double_mix(lo, hi):
-            src = mix_rows[:, lo:hi].rearrange("p a e -> p (a e)").unsqueeze(2).to_broadcast([P, (hi - lo) * E, 2])
-            nc.scalar.copy(out=mix_twice[:, lo * E : hi * E], in_=src)
+            src = mix_rows[:, lo:hi].rearrange("p a e -> p (a e)").unsqueeze(2).to_broadcast([P, (hi - lo) * 2 * E, 2])
+            nc.scalar.copy(out=mix_twice[:, lo * 2 * E : hi * 2 * E], in_=src)
 
 
         def weigh(pair):
@@ -109,7 +121,7 @@ def tile_frozen_fp4_adapter_mix_g1_kernel(tc, x, w, u, mix, b, mag, act, out_0, 
             weights = mix_twice[:, pair * 2 * E : (pair + 1) * 2 * E, :]
             nc.vector.tensor_tensor(
                 out=h[pair][:].rearrange("p (e r i) -> p e r i", r=R // 2, i=2),
-                in0=u_raw[pair][:].rearrange("p a (e r i) -> p (a e) r i", r=R // 2, i=2),
+                in0=xu_raw[pair][:, 2 * K :].rearrange("p (e r i) -> p e r i", r=R // 2, i=2),
                 in1=weights.unsqueeze(2).to_broadcast([P, 2 * E, R // 2, 2]),
                 op=MULT,
             )
@@ -131,18 +143,21 @@ def tile_frozen_fp4_adapter_mix_g1_kernel(tc, x, w, u, mix, b, mag, act, out_0, 
             lay_slab(s, nc.scalar.copy, columns, G)
             lay_slab(s, nc.vector.tensor_copy, 0, columns)
 
-        def quantize(src, name, bufs, width):
+        def mx_tiles(name, bufs, width):
             codes = sb.tile([P, width], U32, name=name + "_codes", bufs=bufs, align_bytes=64)
             scales = sb.tile([P, width], U8, name=name + "_scales", bufs=bufs, align_bytes=64)
-            nc.vector.quantize_mx(out=codes[:].bitcast(FP8X4), scales=scales[:], in_=src)
             return codes, scales
 
         def quantize_slabs(s):
             n = 1 if s < 2 * PASSES else 2
+            if s % 2 == 0:
+                w_two[s] = mx_tiles("w", PASSES, 2 * G)
+            codes, scales = w_two[s - s % 2]
+            cols = slice(s % 2 * G, (s % 2 + n) * G)
             src = w_joint[s][:].rearrange("p c n t -> p (c n t)")
-            codes, scales = quantize(src, "w%d" % n, 2 * PASSES // n, n * G)
-            for k in range(n):
-                w_mx[s + k] = codes[:, k * G : (k + 1) * G], scales[:, k * G : (k + 1) * G]
+            nc.vector.quantize_mx(out=codes[:, cols].bitcast(FP8X4), scales=scales[:, cols], in_=src)
+            for k in range(s % 2, s % 2 + n):
+                w_mx[s - s % 2 + k] = codes[:, k * G : (k + 1) * G], scales[:, k * G : (k + 1) * G]
 
         def prepare_x(a):
             x_side[a] = sb.tile([P, PASSES * P * 4], BF16, name="x_side", bufs=2, align_bytes=64)
@@ -152,7 +167,8 @@ def tile_frozen_fp4_adapter_mix_g1_kernel(tc, x, w, u, mix, b, mag, act, out_0, 
                 for i in range(2):
                     c = 2 * half + i
                     if c < PASSES - 1:
-                        words = x_raw[a][:].bitcast(F32)[:, c * G // 2 : (c + 1) * G // 2]
+                        first = (a % 2 * K + c * G) // 2
+                        words = xu_raw[a // 2][:].bitcast(F32)[:, first : first + G // 2]
                     else:
                         words = h[a // 2][:].bitcast(F32)[:, a % 2 * G // 2 : (a % 2 + 1) * G // 2]
                     for e in range(2):
@@ -160,7 +176,9 @@ def tile_frozen_fp4_adapter_mix_g1_kernel(tc, x, w, u, mix, b, mag, act, out_0, 
                 nc.scalar.copy(out=dst[:, 2 * half : 2 * half + 2], in_=t[:].rearrange("p c e r -> p c r e"))
 
         def quantize_x(a):
-            x_mx[a] = quantize(x_side[a][:], "x", TILES, G)
+            codes, scales = mx_tiles("x", TILES, G)
+            nc.vector.quantize_mx(out=codes[:].bitcast(FP8X4), scales=scales[:], in_=x_side[a][:])
+            x_mx[a] = codes, scales
 
 
         def gate_columns(j, engine, lo, hi):
@@ -201,57 +219,54 @@ def tile_frozen_fp4_adapter_mix_g1_kernel(tc, x, w, u, mix, b, mag, act, out_0, 
 
         def finish(j, i):
             if i == 0:
-                y[j] = sb.tile([P, 2, G], F32, name="y", bufs=10)
+                y[j] = sb.tile([P, 2, G], F32, name="y", bufs=12)
             nc.vector.tensor_tensor(out=y[j][:, i, :], in0=total[j, i][:], in1=gate[j][:, i, :], op=MULT)
 
         def store_y(j):
             g, pair = divmod(j, PAIRS)
-            rows = out_0[pair * 2 * P : (pair + 1) * 2 * P, g * G : (g + 1) * G]
-            nc.sync.dma_start(out=rows.rearrange("(a p) n -> p a n", p=P), in_=y[j][:])
+            nc.sync.dma_start(out=pair_rows(out_0, pair)[:, :, g * G : (g + 1) * G], in_=y[j][:])
 
 
-        def round_y(src, tiles, copy):
-            t = sb.tile([P, 2, tiles * P, 2], BF16, name="y_bf", bufs=4)
+        def round_y(j, lo, hi, copy):
+            if lo == 0:
+                y_bf[j] = sb.tile([P, 2, 2 * P, 2], BF16, name="y_bf", bufs=4)
             copy(
-                out=t[:].rearrange("q e (r s) i -> q r e s i", s=RUN),
-                in_=src.rearrange("q (r s e i) -> q r e s i", s=RUN, e=2, i=2),
+                out=y_bf[j][:, :, lo * P : hi * P, :].rearrange("q e (r s) i -> q r e s i", s=RUN),
+                in_=y[j][:, lo:hi, :].rearrange("q a (r s e i) -> q (a r) e s i", s=RUN, e=2, i=2),
             )
-            return t
-
-        def turn_y(rounded, tiles, k):
-            t = bank(k, [P, tiles, 2, P])
-            words = rounded[:].rearrange("q e r i -> q (e r i)").bitcast(F32)
-            for a in range(tiles):
-                for e in range(2):
-                    first = (tiles * e + a) * P
-                    nc.tensor.transpose(t[:, a, e, :], words[:, first : first + P], ident[:])
-            return t
-
-        def empty_y(t, j, first, tiles):
-            if j not in y_side:
-                y_side[j] = sb.tile([P, 4 * P * 4], BF16, name="y_side", bufs=3, align_bytes=64)
-            dst = y_side[j][:, first * P * 4 : (first + tiles) * P * 4].bitcast(F32)
-            nc.scalar.copy(out=dst.rearrange("p (a r e) -> p a r e", a=tiles, e=2), in_=t[:].rearrange("p a e r -> p a r e"))
-
-        def quantize_y(j, first, tiles):
-            g, pair = divmod(j, PAIRS)
-            if g not in y_codes:
-                y_codes[g] = sb.tile([P, M], U32, name="y_codes", bufs=2, align_bytes=64)
-                if g % 2 == 0:
-                    y_scales[g] = sb.tile([P, M], U8, name="y_scales", bufs=2, align_bytes=64)
-            cols = slice((2 * pair + first) * P, (2 * pair + first + tiles) * P)
-            src = y_side[j][:, first * P * 4 : (first + tiles) * P * 4]
-            nc.vector.quantize_mx(out=y_codes[g][:, cols].bitcast(FP8X4), scales=y_scales[g - g % 2][4 * (g % 2) :, cols], in_=src)
 
         def round_step(j):
             copy = nc.vector.tensor_copy if j >= LAST - 2 else nc.scalar.copy
-            y_bf[j] = round_y(y[j][:].rearrange("q a n -> q (a n)"), 2, copy)
+            if j == LAST:
+                round_y(j, 0, 1, copy)
+                round_y(j, 1, 2, copy)
+            else:
+                round_y(j, 0, 2, copy)
 
         def turn_step(j):
-            y_bank[j] = turn_y(y_bf[j], 2, SUM_BANKS + j % 2)
+            y_bank[j] = bank(SUM_BANKS + j % 2, [P, 2, 2, P])
+            words = y_bf[j][:].rearrange("q e r i -> q (e r i)").bitcast(F32)
+            for a in range(2):
+                for e in range(2):
+                    first = (2 * e + a) * P
+                    nc.tensor.transpose(y_bank[j][:, a, e, :], words[:, first : first + P], ident[:])
 
         def empty_step(j):
-            empty_y(y_bank[j], j - j % 2, 2 * (j % 2), 2)
+            if j % 2 == 0:
+                y_side[j] = sb.tile([P, 2, 2 * P * 4], BF16, name="y_side", bufs=3, align_bytes=64)
+            dst = y_side[j - j % 2][:, j % 2, :].bitcast(F32).rearrange("p (r a e) -> p r a e", a=2, e=2)
+            nc.scalar.copy(out=dst, in_=y_bank[j][:].rearrange("p a e r -> p r a e"))
+
+        def quantize_y(j, steps):
+            g, pair = divmod(j, PAIRS)
+            if pair == 0:
+                y_codes[g] = sb.tile([P, M], U32, name="y_codes", bufs=2, align_bytes=64)
+                if g % 2 == 0:
+                    y_scales[g] = sb.tile([P, M], U8, name="y_scales", bufs=2, align_bytes=64)
+            cols = slice(pair * 2 * P, (pair + steps) * 2 * P)
+            src = y_side[j - j % 2][:, j % 2 : j % 2 + steps, :].rearrange("p k v -> p (k v)")
+            scales = y_scales[g - g % 2][4 * (g % 2) :, cols]
+            nc.vector.quantize_mx(out=y_codes[g][:, cols].bitcast(FP8X4), scales=scales, in_=src)
 
         def store_words(j, steps):
             g, pair = divmod(j, PAIRS)
@@ -266,14 +281,14 @@ def tile_frozen_fp4_adapter_mix_g1_kernel(tc, x, w, u, mix, b, mag, act, out_0, 
         make_identity(nc, ident[:])
         nc.sync.dma_start(out=mag_rows[:], in_=mag.rearrange("(p c) -> p c", p=P))
         load_slab(0)
-        load_mix(0, 2)
+        load_mix(0, 1)
         load_u(0)
         load_x(0)
         load_act(0)
         for s in range(1, PASSES):
             load_slab(s)
         load_x(1)
-        load_mix(2, TILES)
+        load_mix(1, PAIRS)
         for pair in range(1, PAIRS):
             load_u(pair)
             load_x(2 * pair)
@@ -283,13 +298,10 @@ def tile_frozen_fp4_adapter_mix_g1_kernel(tc, x, w, u, mix, b, mag, act, out_0, 
         load_slab(2 * PASSES - 1)
         load_act(PAIRS)
         load_act(PAIRS + 1)
-        load_slab(2 * PASSES)
-        load_act(PAIRS + 2)
-        load_act(PAIRS + 3)
 
         mag_banks = [turn_mag(k) for k in range(2)]
         share_slab(0, VECTOR_HALF)
-        double_mix(0, 2)
+        double_mix(0, 1)
         for k in range(2):
             spread_mag(k, mag_banks[k])
         weigh(0)
@@ -304,7 +316,7 @@ def tile_frozen_fp4_adapter_mix_g1_kernel(tc, x, w, u, mix, b, mag, act, out_0, 
         share_slab(3, VECTOR_HALF)
         quantize_slabs(2)
         quantize_slabs(3)
-        double_mix(2, TILES)
+        double_mix(1, PAIRS)
 
         def lay_half(n):
             s = PASSES + n // 2
@@ -318,8 +330,6 @@ def tile_frozen_fp4_adapter_mix_g1_kernel(tc, x, w, u, mix, b, mag, act, out_0, 
 
         for a in range(TILES):
             j, i = divmod(a, 2)
-            if i == 1 and j > 0:
-                load_slab(2 * PASSES + j)
             if a + 1 < TILES:
                 prepare_x(a + 1)
             multiply(j, [i], range(2 if a == 0 else 0, PASSES))
@@ -336,6 +346,10 @@ def tile_frozen_fp4_adapter_mix_g1_kernel(tc, x, w, u, mix, b, mag, act, out_0, 
                 quantize_x(a + 1)
             if a > 0:
                 lay_half(a - 1)
+        for c in range(PASSES):
+            load_two_slabs(c)
+            if c in (1, 2):
+                load_act(PAIRS + 1 + c)
         lay_half(TILES - 1)
         quantize_slabs(2 * PASSES - 1)
         make_gate(PAIRS)
@@ -353,8 +367,6 @@ def tile_frozen_fp4_adapter_mix_g1_kernel(tc, x, w, u, mix, b, mag, act, out_0, 
             ahead = j + (ACT_LEAD_ODD if j % 2 == 0 else ACT_LEAD_EVEN)
             if ahead < STEPS:
                 load_act(ahead)
-            if s + PASSES < SLABS:
-                load_slab(s + PASSES)
             if j % 2 == 0:
                 make_gate_gpsimd(j + 1)
             early, late = range(PASSES // 2), range(PASSES // 2, PASSES)
@@ -388,7 +400,7 @@ def tile_frozen_fp4_adapter_mix_g1_kernel(tc, x, w, u, mix, b, mag, act, out_0, 
                     quantize_slabs(s - 1)
                 ready = rounded_at[j - 3][:1] + rounded_at[j - 2][:1]
                 for q in ready:
-                    quantize_y(q, 0, 4)
+                    quantize_y(q, 2)
                 if j < LAST:
                     make_gate(j + 1)
             while stored < min(j, j - PAIRS + 1 + max(0, j - 2 * PAIRS)):
@@ -402,22 +414,19 @@ def tile_frozen_fp4_adapter_mix_g1_kernel(tc, x, w, u, mix, b, mag, act, out_0, 
         round_step(LAST - 1)
         for i in range(2):
             finish(LAST, i)
-            a = TILES - 2 + i
-            nc.sync.dma_start(out=out_0[a * P : (a + 1) * P, N - G :], in_=y[LAST][:, i, :])
+            nc.sync.dma_start(out=pair_rows(out_0, PAIRS - 1)[:, i, N - G :], in_=y[LAST][:, i, :])
         for q in rounded_at[LAST]:
             turn_step(q)
             empty_step(q)
         turn_step(LAST - 1)
-        last_banks = [turn_y(round_y(y[LAST][:, i, :], 1, nc.vector.tensor_copy), 1, i) for i in range(2)]
         empty_step(LAST - 1)
-        for i in range(2):
-            empty_y(last_banks[i], LAST - 1, 2 + i, 1)
+        round_step(LAST)
+        turn_step(LAST)
+        empty_step(LAST)
         for q in rounded_at[LAST - 1][:1] + rounded_at[LAST][:1]:
-            quantize_y(q, 0, 4)
+            quantize_y(q, 2)
             store_words(q, 2)
-        quantize_y(LAST - 1, 0, 2)
-        store_words(LAST - 1, 1)
-        for i in range(2):
-            quantize_y(LAST - 1, 2 + i, 1)
-        store_words(LAST, 1)
+        for q in (LAST - 1, LAST):
+            quantize_y(q, 1)
+            store_words(q, 1)
         store_scales(2)

from contextlib import ExitStack

import concourse.mybir as mybir
from concourse.masks import make_identity

M, K, N, E, R = 1024, 1536, 2048, 16, 32
FLOPS = 2 * M * (K + E * R) * N

F32 = mybir.dt.float32
BF16 = mybir.dt.bfloat16
U32 = mybir.dt.uint32
I32 = mybir.dt.int32
U8 = mybir.dt.uint8
FP8X4 = mybir.dt.float8_e4m3fn_x4
MULT = mybir.AluOpType.mult

P = 128
G = 512
PASSES = (K + E * R) // G
CHUNKS = N // G
TILES = M // P
PAIRS = TILES // 2
STEPS = CHUNKS * PAIRS
SLABS = CHUNKS * PASSES
LAST = STEPS - 1
RUN = 4

VECTOR_HALF = 256
VECTOR_FIRST = 64
VECTOR_LATER = 352
GPSIMD_COLUMNS = 416
PLANES_FROM = 6
ACT_LEAD_EVEN, ACT_LEAD_ODD = 3, 5
SUM_BANKS = 6


def tile_frozen_fp4_adapter_mix_g1_kernel(tc, x, w, u, mix, b, mag, act, out_0, out_1, out_2):
    nc = tc.nc
    with ExitStack() as ctx:
        sb = ctx.enter_context(tc.tile_pool(name="sb", bufs=1))
        ps = ctx.enter_context(tc.psum_pool(name="ps", bufs=1))
        ctx.enter_context(tc.manual_schedule())

        ident = sb.tile([P, P], F32, name="ident")
        mag_rows = sb.tile([P, N // P], BF16, name="mag_rows")
        mag_all = sb.tile([P, N], BF16, name="mag_all")
        mix_rows = sb.tile([P, PAIRS, 2 * E], BF16, name="mix_rows")
        mix_twice = sb.tile([P, TILES * E, 2], BF16, name="mix_twice")
        words_out = out_1.rearrange("g p m t -> g p (m t)").bitcast(I32)
        scales_out = out_2.bitcast(I32)

        xu_raw, h, act_sb, x_side, x_mx = {}, {}, {}, {}, {}
        w_raw, w_side, w_joint, w_two, w_mx = {}, {}, {}, {}, {}
        gate, total, y, y_bf, y_bank, y_side, y_codes, y_scales = {}, {}, {}, {}, {}, {}, {}, {}

        def bank(k, shape):
            return ps.tile(shape, F32, name="bank", tag="bank%d" % k)


        def pair_rows(t, pair):
            return t[pair * 2 * P : (pair + 1) * 2 * P, :].rearrange("(p i) n -> p i n", i=2)

        def pass_rows(c):
            rows = w[c * G : (c + 1) * G, :] if c < PASSES - 1 else b
            return rows.rearrange("(p t) n -> p t n", t=4)

        def load_slab(s):
            g, c = divmod(s, PASSES)
            t = sb.tile([P, 4, G], BF16, name="w_raw", bufs=4)
            nc.sync.dma_start(out=t[:], in_=pass_rows(c)[:, :, g * G : (g + 1) * G])
            w_raw[s] = t[:]

        def load_two_slabs(c):
            t = sb.tile([P, 4, 2 * G], BF16, name="w_wide", tag="wide%d" % c)
            nc.sync.dma_start(out=t[:], in_=pass_rows(c)[:, :, 2 * G :])
            w_raw[2 * PASSES + c], w_raw[3 * PASSES + c] = t[:, :, :G], t[:, :, G:]

        def load_u(pair):
            xu_raw[pair] = sb.tile([P, 2 * (K + G)], BF16, name="xu_raw", tag="wide%d" % pair)
            dst = xu_raw[pair][:, 2 * K :].rearrange("p (i r) -> p i r", i=2)
            nc.sync.dma_start(out=dst, in_=pair_rows(u, pair))

        def load_x(a):
            pair, i = divmod(a, 2)
            nc.sync.dma_start(out=xu_raw[pair][:, i * K : (i + 1) * K], in_=pair_rows(x, pair)[:, i, :])

        def load_mix(lo, hi):
            src = mix[lo * 2 * P : hi * 2 * P, :].rearrange("(c p i) e -> p c (i e)", p=P, i=2)
            nc.sync.dma_start(out=mix_rows[:, lo:hi], in_=src)

        def shared_tag(j):
            return "shared%d" % (j // 2 % 3)

        def load_act(j):
            g, pair = divmod(j, PAIRS)
            if j >= PAIRS and j % 2 == 0:
                act_sb[j] = sb.tile([P, 2, G], BF16, name="act_even", tag=shared_tag(j))
            else:
                act_sb[j] = sb.tile([P, 2, G], BF16, name="act_other", bufs=4)
            nc.sync.dma_start(out=act_sb[j][:], in_=pair_rows(act, pair)[:, :, g * G : (g + 1) * G])


        def turn_mag(k):
            words = mag_rows[:].bitcast(F32)
            t = bank(4 + k, [P, 4, P])
            for i in range(4):
                nc.tensor.transpose(t[:, i, :], words[:, 4 * k + i : 4 * k + i + 1].to_broadcast([P, P]), ident[:])
            return t

        def spread_mag(k, t):
            dst = mag_all[:].bitcast(F32).rearrange("q (p k i) -> q k p i", k=2, i=4)
            nc.scalar.copy(out=dst[:, k], in_=t[:].rearrange("q i p -> q p i"))

        def double_mix(lo, hi):
            src = mix_rows[:, lo:hi].rearrange("p a e -> p (a e)").unsqueeze(2).to_broadcast([P, (hi - lo) * 2 * E, 2])
            nc.scalar.copy(out=mix_twice[:, lo * 2 * E : hi * 2 * E], in_=src)


        def weigh(pair):
            h[pair] = sb.tile([P, 2 * G], BF16, name="h", bufs=2)
            weights = mix_twice[:, pair * 2 * E : (pair + 1) * 2 * E, :]
            nc.vector.tensor_tensor(
                out=h[pair][:].rearrange("p (e r i) -> p e r i", r=R // 2, i=2),
                in0=xu_raw[pair][:, 2 * K :].rearrange("p (e r i) -> p e r i", r=R // 2, i=2),
                in1=weights.unsqueeze(2).to_broadcast([P, 2 * E, R // 2, 2]),
                op=MULT,
            )

        def lay_slab(s, copy, lo, hi):
            if s not in w_side:
                if s < 2 * PASSES:
                    w_joint[s] = sb.tile([P, 1, G, 4], BF16, name="w_side", tag="side%d" % (s % 2), align_bytes=64)
                else:
                    w_joint[s] = sb.tile([P, 2, G, 4], BF16, name="w_side", tag="side%d" % (s // 2 % 2), align_bytes=64)
                    w_side[s + 1] = w_joint[s][:, 1]
                w_side[s] = w_joint[s][:, 0]
            copy(
                out=w_side[s][:, lo:hi, :].rearrange("p (c i) t -> p c t i", i=RUN),
                in_=w_raw[s][:, :, lo:hi].rearrange("p t (c i) -> p c t i", i=RUN),
            )

        def share_slab(s, columns):
            lay_slab(s, nc.scalar.copy, columns, G)
            lay_slab(s, nc.vector.tensor_copy, 0, columns)

        def mx_tiles(name, bufs, width):
            codes = sb.tile([P, width], U32, name=name + "_codes", bufs=bufs, align_bytes=64)
            scales = sb.tile([P, width], U8, name=name + "_scales", bufs=bufs, align_bytes=64)
            return codes, scales

        def quantize_slabs(s):
            n = 1 if s < 2 * PASSES else 2
            if s % 2 == 0:
                w_two[s] = mx_tiles("w", PASSES, 2 * G)
            codes, scales = w_two[s - s % 2]
            cols = slice(s % 2 * G, (s % 2 + n) * G)
            src = w_joint[s][:].rearrange("p c n t -> p (c n t)")
            nc.vector.quantize_mx(out=codes[:, cols].bitcast(FP8X4), scales=scales[:, cols], in_=src)
            for k in range(s % 2, s % 2 + n):
                w_mx[s - s % 2 + k] = codes[:, k * G : (k + 1) * G], scales[:, k * G : (k + 1) * G]

        def prepare_x(a):
            x_side[a] = sb.tile([P, PASSES * P * 4], BF16, name="x_side", bufs=2, align_bytes=64)
            dst = x_side[a][:].bitcast(F32).rearrange("p (c r e) -> p c r e", c=PASSES, e=2)
            for half in range(2):
                t = bank(4 + (2 * a + half + 2) % 4, [P, 2, 2, P])
                for i in range(2):
                    c = 2 * half + i
                    if c < PASSES - 1:
                        first = (a % 2 * K + c * G) // 2
                        words = xu_raw[a // 2][:].bitcast(F32)[:, first : first + G // 2]
                    else:
                        words = h[a // 2][:].bitcast(F32)[:, a % 2 * G // 2 : (a % 2 + 1) * G // 2]
                    for e in range(2):
                        nc.tensor.transpose(t[:, i, e, :], words[:, e::2], ident[:])
                nc.scalar.copy(out=dst[:, 2 * half : 2 * half + 2], in_=t[:].rearrange("p c e r -> p c r e"))

        def quantize_x(a):
            codes, scales = mx_tiles("x", TILES, G)
            nc.vector.quantize_mx(out=codes[:].bitcast(FP8X4), scales=scales[:], in_=x_side[a][:])
            x_mx[a] = codes, scales


        def gate_columns(j, engine, lo, hi):
            g = j // PAIRS
            engine.tensor_tensor(
                out=gate[j][:, :, lo:hi],
                in0=act_sb[j][:, :, lo:hi],
                in1=mag_all[:, g * G + lo : g * G + hi].unsqueeze(1).to_broadcast([P, 2, hi - lo]),
                op=MULT,
            )

        def make_gate(j):
            gate[j] = sb.tile([P, 2, G], F32, name="gate", bufs=2)
            gate_columns(j, nc.vector, 0, G)

        def make_gate_gpsimd(j):
            gate[j] = sb.tile([P, 2, G], F32, name="gate_odd", tag=shared_tag(j - 1))
            gate_columns(j, nc.gpsimd, 0, GPSIMD_COLUMNS)

        def multiply(j, tiles, passes):
            g, pair = divmod(j, PAIRS)
            for c in passes:
                w_codes, w_scales = w_mx[g * PASSES + c]
                for i in tiles:
                    if c == 0:
                        n = 2 * j + i
                        total[j, i] = bank(n % 4 if n < TILES else (n - TILES + 4) % SUM_BANKS, [P, G])
                    x_codes, x_scales = x_mx[2 * pair + i]
                    nc.tensor.matmul_mx(
                        out=total[j, i][:],
                        lhsT=x_codes[:, c * P : (c + 1) * P].bitcast(FP8X4),
                        lhsT_scale=x_scales[:, c * P : (c + 1) * P],
                        rhs=w_codes.bitcast(FP8X4),
                        rhs_scale=w_scales,
                        start=(c == 0),
                        stop=(c == PASSES - 1),
                    )

        def finish(j, i):
            if i == 0:
                y[j] = sb.tile([P, 2, G], F32, name="y", bufs=12)
            nc.vector.tensor_tensor(out=y[j][:, i, :], in0=total[j, i][:], in1=gate[j][:, i, :], op=MULT)

        def store_y(j):
            g, pair = divmod(j, PAIRS)
            nc.sync.dma_start(out=pair_rows(out_0, pair)[:, :, g * G : (g + 1) * G], in_=y[j][:])


        def round_y(j, lo, hi, copy):
            if lo == 0:
                y_bf[j] = sb.tile([P, 2, 2 * P, 2], BF16, name="y_bf", bufs=4)
            copy(
                out=y_bf[j][:, :, lo * P : hi * P, :].rearrange("q e (r s) i -> q r e s i", s=RUN),
                in_=y[j][:, lo:hi, :].rearrange("q a (r s e i) -> q (a r) e s i", s=RUN, e=2, i=2),
            )

        def round_step(j):
            copy = nc.vector.tensor_copy if j >= LAST - 2 else nc.scalar.copy
            if j == LAST:
                round_y(j, 0, 1, copy)
                round_y(j, 1, 2, copy)
            else:
                round_y(j, 0, 2, copy)

        def turn_step(j):
            y_bank[j] = bank(SUM_BANKS + j % 2, [P, 2, 2, P])
            words = y_bf[j][:].rearrange("q e r i -> q (e r i)").bitcast(F32)
            for a in range(2):
                for e in range(2):
                    first = (2 * e + a) * P
                    nc.tensor.transpose(y_bank[j][:, a, e, :], words[:, first : first + P], ident[:])

        def empty_step(j):
            if j % 2 == 0:
                y_side[j] = sb.tile([P, 2, 2 * P * 4], BF16, name="y_side", bufs=3, align_bytes=64)
            dst = y_side[j - j % 2][:, j % 2, :].bitcast(F32).rearrange("p (r a e) -> p r a e", a=2, e=2)
            nc.scalar.copy(out=dst, in_=y_bank[j][:].rearrange("p a e r -> p r a e"))

        def quantize_y(j, steps):
            g, pair = divmod(j, PAIRS)
            if pair == 0:
                y_codes[g] = sb.tile([P, M], U32, name="y_codes", bufs=2, align_bytes=64)
                if g % 2 == 0:
                    y_scales[g] = sb.tile([P, M], U8, name="y_scales", bufs=2, align_bytes=64)
            cols = slice(pair * 2 * P, (pair + steps) * 2 * P)
            src = y_side[j - j % 2][:, j % 2 : j % 2 + steps, :].rearrange("p k v -> p (k v)")
            scales = y_scales[g - g % 2][4 * (g % 2) :, cols]
            nc.vector.quantize_mx(out=y_codes[g][:, cols].bitcast(FP8X4), scales=scales, in_=src)

        def store_words(j, steps):
            g, pair = divmod(j, PAIRS)
            cols = slice(pair * 2 * P, (pair + steps) * 2 * P)
            nc.sync.dma_start(out=words_out[g, :, cols], in_=y_codes[g][:, cols].bitcast(I32))

        def store_scales(g):
            for q in range(4):
                src = y_scales[g][32 * q : 32 * q + 8, :].bitcast(I32)
                nc.sync.dma_start(out=scales_out[g : g + 2, 4 * q : 4 * q + 4, :], in_=src)

        make_identity(nc, ident[:])
        nc.sync.dma_start(out=mag_rows[:], in_=mag.rearrange("(p c) -> p c", p=P))
        load_slab(0)
        load_mix(0, 1)
        load_u(0)
        load_x(0)
        load_act(0)
        for s in range(1, PASSES):
            load_slab(s)
        load_x(1)
        load_mix(1, PAIRS)
        for pair in range(1, PAIRS):
            load_u(pair)
            load_x(2 * pair)
            load_slab(PASSES + pair - 1)
            load_x(2 * pair + 1)
            load_act(pair)
        load_slab(2 * PASSES - 1)
        load_act(PAIRS)
        load_act(PAIRS + 1)

        mag_banks = [turn_mag(k) for k in range(2)]
        share_slab(0, VECTOR_HALF)
        double_mix(0, 1)
        for k in range(2):
            spread_mag(k, mag_banks[k])
        weigh(0)
        quantize_slabs(0)
        prepare_x(0)
        make_gate(0)
        share_slab(1, VECTOR_HALF)
        quantize_x(0)
        quantize_slabs(1)
        multiply(0, [0], range(2))
        share_slab(2, VECTOR_HALF)
        share_slab(3, VECTOR_HALF)
        quantize_slabs(2)
        quantize_slabs(3)
        double_mix(1, PAIRS)

        def lay_half(n):
            s = PASSES + n // 2
            share = VECTOR_FIRST if s + 1 < 2 * PASSES else VECTOR_HALF
            middle = (share + G) // 2
            if n % 2 == 0:
                lay_slab(s, nc.scalar.copy, share, middle)
            else:
                lay_slab(s, nc.scalar.copy, middle, G)
                lay_slab(s, nc.vector.tensor_copy, 0, share)

        for a in range(TILES):
            j, i = divmod(a, 2)
            if a + 1 < TILES:
                prepare_x(a + 1)
            multiply(j, [i], range(2 if a == 0 else 0, PASSES))
            if 0 < a < TILES - 1:
                finish((a - 1) // 2, (a - 1) % 2)
            if i == 0:
                if j + 1 < PAIRS:
                    weigh(j + 1)
                if j > 0:
                    make_gate(j)
            elif j > 0:
                quantize_slabs(PASSES + j - 1)
            if a + 1 < TILES:
                quantize_x(a + 1)
            if a > 0:
                lay_half(a - 1)
        for c in range(PASSES):
            load_two_slabs(c)
            if c in (1, 2):
                load_act(PAIRS + 1 + c)
        lay_half(TILES - 1)
        quantize_slabs(2 * PASSES - 1)
        make_gate(PAIRS)

        rounded_at = {j: [] for j in range(STEPS)}
        done = 0
        for j in range(PLANES_FROM, STEPS):
            if j % 2 == 0 or j >= STEPS - PAIRS:
                rounded_at[j] = [done, done + 1]
                done = done + 2

        stored = 0
        for j in range(PAIRS, STEPS):
            s = j + PASSES
            ahead = j + (ACT_LEAD_ODD if j % 2 == 0 else ACT_LEAD_EVEN)
            if ahead < STEPS:
                load_act(ahead)
            if j % 2 == 0:
                make_gate_gpsimd(j + 1)
            early, late = range(PASSES // 2), range(PASSES // 2, PASSES)
            if j == LAST:
                multiply(j, [0], range(PASSES))
            elif j % PAIRS != 1:
                multiply(j, [0, 1], early)
            for q in rounded_at[j - 1]:
                turn_step(q)
            if j % PAIRS == 0:
                multiply(j + 1, [0, 1], early)
            if j == LAST:
                multiply(j, [1], range(PASSES))
            else:
                multiply(j, [0, 1], late)
            finish(j - 1, 0)
            finish(j - 1, 1)
            for q in rounded_at[j]:
                round_step(q)
            if s < SLABS:
                if j % 2 == 0:
                    lay_slab(s, nc.scalar.copy, 0, G)
                else:
                    share_slab(s, VECTOR_LATER)
            for q in rounded_at[j - 1]:
                empty_step(q)
            ready = []
            if j % 2 == 1:
                gate_columns(j, nc.vector, GPSIMD_COLUMNS, G)
                if s < SLABS:
                    quantize_slabs(s - 1)
                ready = rounded_at[j - 3][:1] + rounded_at[j - 2][:1]
                for q in ready:
                    quantize_y(q, 2)
                if j < LAST:
                    make_gate(j + 1)
            while stored < min(j, j - PAIRS + 1 + max(0, j - 2 * PAIRS)):
                store_y(stored)
                stored = stored + 1
            for q in ready:
                store_words(q, 2)
                if q == 2 * PAIRS - 2:
                    store_scales(0)

        round_step(LAST - 1)
        for i in range(2):
            finish(LAST, i)
            nc.sync.dma_start(out=pair_rows(out_0, PAIRS - 1)[:, i, N - G :], in_=y[LAST][:, i, :])
        for q in rounded_at[LAST]:
            turn_step(q)
            empty_step(q)
        turn_step(LAST - 1)
        empty_step(LAST - 1)
        round_step(LAST)
        turn_step(LAST)
        empty_step(LAST)
        for q in rounded_at[LAST - 1][:1] + rounded_at[LAST][:1]:
            quantize_y(q, 2)
            store_words(q, 2)
        for q in (LAST - 1, LAST):
            quantize_y(q, 1)
            store_words(q, 1)
        store_scales(2)
